import numpy as np
import ml_dtypes


def mxq(x, axis, fmt="e4m3"):
    dtype, down = {"e4m3": (ml_dtypes.float8_e4m3fn, 7), "e5m2": (ml_dtypes.float8_e5m2, 14)}[fmt]
    v = np.moveaxis(np.asarray(x, np.float32).astype(ml_dtypes.bfloat16).astype(np.float64), axis, -1)
    blocks = v.reshape(v.shape[:-1] + (-1, 32))
    amax = np.abs(blocks).max(-1, keepdims=True)
    byte = np.maximum(np.where(amax > 0, np.frexp(amax)[1] - 1 + 127, 0) - down, 1)
    scale = np.exp2(byte - 127.0)
    codes = (blocks / scale).astype(np.float32).astype(dtype).astype(np.float64)
    return np.moveaxis((codes * scale).reshape(v.shape), -1, axis)


WIDE = False


def mx_kscale(k):
    if not WIDE:
        return np.ones(k)
    levels = np.array([10, -10, 5, -5, 0])
    if k % 512:
        return np.exp2(np.random.permutation(np.resize(levels, k // 32))).repeat(32)
    a = np.empty((k // 512, 16))
    for p in range(k // 512):
        a[p, :8] = np.random.permutation(np.resize(levels, 8))
        for g in range(8):
            far = levels[np.abs(levels - a[p, g]) >= 10]
            a[p, g + 8] = far[np.random.randint(len(far))]
    return np.exp2(a.ravel()).repeat(32)


def f64(x):
    return np.asarray(x).astype(np.float64)


def striped(idx):
    return np.tile(np.asarray(idx).reshape(-1, 16).T, (8, 1)).astype(np.uint16)


def unstriped(offs):
    return offs[:16].T.reshape(-1).astype(np.int64)


E2M1 = np.array([0.0, 0.5, 1.0, 1.5, 2.0, 3.0, 4.0, 6.0, -0.0, -0.5, -1.0, -1.5, -2.0, -3.0, -4.0, -6.0])


def pack_weight(w, fmt):
    k, n = w.shape
    w = f64(np.asarray(w, np.float32).astype(ml_dtypes.bfloat16)).reshape(k // 32, 32, n)
    amax = np.abs(w).max(1)
    if fmt == "e4m3":
        byte = np.frexp(amax)[1] - 1 + 127 - 7
    else:
        mant, ex = np.frexp(amax / 6.0)
        byte = np.where(mant > 0.5, ex, ex - 1) + 127
    byte = np.clip(np.where(amax > 0, byte, 1), 1, 254)
    scaled = (w * np.exp2(127.0 - byte)[:, None, :]).reshape(k, n).astype(np.float32)
    by_word = np.ascontiguousarray(scaled.reshape(k // 512, 128, 4, n).transpose(0, 1, 3, 2))
    if fmt == "e4m3":
        words = by_word.astype(ml_dtypes.float8_e4m3fn).view(np.uint8)
    else:
        c = by_word.astype(ml_dtypes.float4_e2m1fn).view(np.uint8) & 0xF
        words = (c[..., 0::2] | (c[..., 1::2] << 4)).reshape(k // 512, 128, 2 * n)
    return np.ascontiguousarray(words), np.ascontiguousarray(byte.astype(np.uint8).reshape(k // 512, 16, n))


def unpack_weight(words, scales, fmt):
    g, _, n = scales.shape
    words = np.ascontiguousarray(words).reshape(g, 128, n, -1)
    if fmt == "e4m3":
        vals = words.view(ml_dtypes.float8_e4m3fn).astype(np.float64)
    else:
        nib = np.empty((g, 128, n, 4), np.uint8)
        nib[..., 0::2] = words & 0xF
        nib[..., 1::2] = words >> 4
        vals = E2M1[nib]
    vals = vals * np.repeat(np.exp2(scales.astype(np.float64) - 127.0), 8, axis=1)[..., None]
    return vals.transpose(0, 1, 3, 2).reshape(g * 512, n)


K, U, I, T, E = 512, 2048, 512, 1024, 512


def setup_inputs():
    n = np.random.standard_normal
    idx = np.random.permutation(U)[:I]
    idx2 = np.random.permutation(T)[:I]
    fk = mx_kscale(K)
    embp = pack_weight(n((K, U)) / fk[:, None], "e4m3")
    return {
        "emb_words": embp[0],
        "emb_scales": embp[1],
        "wv": (n((K, E)) * 1 / np.sqrt(K) * fk[:, None]).astype(np.float32),
        "old": (n((E, T))).astype(np.float32),
        "retain": (np.random.uniform(0.0, 1.0, (1, T))).astype(np.float32),
        "offs": striped(idx),
        "offs2": striped(idx2),
    }


def reference(emb_words, emb_scales, wv, old, retain, offs, offs2):
    idx = unstriped(offs)
    idx2 = unstriped(offs2)
    embu = unpack_weight(emb_words, emb_scales, "e4m3")
    wvq = mxq(f64(wv), 0, "e4m3")
    embidxg = embu[:, idx]
    v = wvq.T @ embidxg
    vf = np.zeros((E, T))
    vf[:, idx2] = v
    y = f64(old) * f64(retain) + vf
    return y

@@ -1,0 +1,192 @@
+from contextlib import ExitStack
+
+import concourse.mybir as mybir
+from concourse.masks import make_identity
+
+K, U, I, T, E = 512, 2048, 512, 1024, 512
+FLOPS = 2 * K * E * I
+
+F32 = mybir.dt.float32
+BF16 = mybir.dt.bfloat16
+I32 = mybir.dt.int32
+U32 = mybir.dt.uint32
+U16 = mybir.dt.uint16
+U8 = mybir.dt.uint8
+FP8X4 = mybir.dt.float8_e4m3fn_x4
+COPY = mybir.ActivationFunctionType.Copy
+MULT = mybir.AluOpType.mult
+ADD = mybir.AluOpType.add
+
+P = 128
+PACK = 4
+BANK = 512
+HALF = I // 2
+E_TILES = E // P
+T_BLOCKS = T // P
+
+
+def interleaved(dst, src):
+    return (
+        dst.rearrange("p (c i) r -> p c r i", i=4),
+        src.rearrange("p r (c i) -> p c r i", i=4),
+    )
+
+
+def tile_attend_cachewrite_kernel(tc, emb_words, emb_scales, wv, old, retain, offs, offs2, out):
+    nc = tc.nc
+    wv_rows = wv.rearrange("(p r) e -> p r e", r=PACK)
+
+    with ExitStack() as ctx:
+        keep = ctx.enter_context(tc.tile_pool(name="keep", bufs=1))
+        v_psum = ctx.enter_context(tc.psum_pool(name="v_psum", bufs=2))
+        turn_psum = ctx.enter_context(tc.psum_pool(name="turn_psum", bufs=2))
+        back_psum = ctx.enter_context(tc.psum_pool(name="back_psum", bufs=4))
+
+        gather_list = keep.tile([P, I // 16], U16, name="gather_list")
+        scatter_list = keep.tile([P, I // 16], U16, name="scatter_list")
+        words = keep.tile([P, U], U32, name="words", align_bytes=64)
+        planes = keep.tile([P, U], U8, name="planes", align_bytes=64)
+        picked_words = keep.tile([P, I], U32, name="picked_words", align_bytes=64)
+        picked_planes = keep.tile([P, I], U8, name="picked_planes", align_bytes=64)
+        w_codes = keep.tile([P, E], U32, name="w_codes", align_bytes=64)
+        w_planes = keep.tile([P, E], U8, name="w_planes", align_bytes=64)
+        identity = keep.tile([P, P], F32, name="identity")
+        retain_rows = keep.tile([P, P], F32, name="retain_rows")
+        retain_cols = keep.tile([P, T_BLOCKS], F32, name="retain_cols")
+        retain_wide = keep.tile([P, T], F32, name="retain_wide")
+        windows = [keep.tile([P, T], F32, name=f"window{j}") for j in range(E_TILES)]
+        olds = [keep.tile([P, T], F32, name=f"old{j}") for j in range(E_TILES)]
+        results = [keep.tile([P, T], F32, name=f"result{j}") for j in range(E_TILES)]
+
+        nc.vector.memset(planes[:].bitcast(I32), 0)
+        nc.gpsimd.memset(retain_rows[:], 0.0)
+        nc.sync.dma_start(out=retain_rows[0:T_BLOCKS, :], in_=retain.rearrange("o (m n) -> (o m) n", n=P))
+        nc.sync.dma_start(gather_list[:], offs)
+        raw0 = keep.tile([P, PACK, P], F32, name="raw0")
+        nc.sync.dma_start(out=raw0[:], in_=wv_rows[:, :, 0:P])
+        for q in range(4):
+            nc.sync.dma_start(
+                out=planes[32 * q : 32 * q + 4, :].bitcast(I32),
+                in_=emb_scales[0, 4 * q : 4 * q + 4, :].bitcast(I32),
+            )
+        nc.sync.dma_start(
+            out=words[:].bitcast(I32),
+            in_=emb_words[0].rearrange("p c r -> p (c r)").bitcast(I32),
+        )
+        nc.sync.dma_start(scatter_list[:], offs2)
+        raw1 = keep.tile([P, PACK, P], F32, name="raw1", tag="stage1")
+        nc.sync.dma_start(out=raw1[:], in_=wv_rows[:, :, P : 2 * P])
+        raw23 = keep.tile([P, PACK, 2 * P], F32, name="raw23", tag="stage23")
+        nc.sync.dma_start(out=raw23[:], in_=wv_rows[:, :, 2 * P : 4 * P])
+        for j in range(E_TILES):
+            nc.sync.dma_start(out=olds[j][:], in_=old[j * P : (j + 1) * P, :])
+
+        make_identity(nc, identity[:])
+        for j in range(E_TILES):
+            nc.vector.memset(windows[j][:], 0.0)
+
+        turned_rows = turn_psum.tile([P, BANK], F32, name="turned", tag="turned")
+        nc.tensor.transpose(turned_rows[:, 0:P], retain_rows[:], identity[:])
+        nc.scalar.activation(retain_cols[:], turned_rows[:, 0:T_BLOCKS], COPY)
+        for h in range(2):
+            spread = back_psum.tile([P, BANK], F32, name="back", tag="back")
+            for b in range(4):
+                m = 4 * h + b
+                nc.tensor.transpose(
+                    spread[:, b * P : (b + 1) * P], retain_cols[:, m : m + 1].to_broadcast([P, P]), identity[:]
+                )
+            nc.scalar.copy(retain_wide[:, h * BANK : (h + 1) * BANK], spread[:])
+
+        def quantise(grouped, cols):
+            nc.vector.quantize_mx(
+                out=w_codes[:, cols].bitcast(FP8X4),
+                scales=w_planes[:, cols],
+                in_=grouped[:].rearrange("p c r -> p (c r)"),
+            )
+
+        def project(j, slots, dst):
+            n = slots.stop - slots.start
+            acc = v_psum.tile([P, BANK], F32, name="acc", tag="acc")
+            nc.tensor.matmul_mx(
+                out=acc[:, 0:n],
+                lhsT=w_codes[:, j * P : (j + 1) * P].bitcast(FP8X4),
+                lhsT_scale=w_planes[:, j * P : (j + 1) * P],
+                rhs=picked_words[:, slots].bitcast(FP8X4),
+                rhs_scale=picked_planes[:, slots],
+                start=True,
+                stop=True,
+            )
+            nc.scalar.copy(dst, acc[:, 0:n])
+
+        def scatter(j, slots, src):
+            cols = slice(slots.start // 16, slots.stop // 16)
+            nc.vector.tensor_copy(windows[j][:].indirect(scatter_list[:, cols]), src)
+
+        def scaled_old(j):
+            banks = []
+            for h in range(2):
+                turned = turn_psum.tile([P, BANK], F32, name="turned", tag="turned")
+                scaled = keep.tile([P, BANK], F32, name="scaled", tag="scaled", bufs=2)
+                back = back_psum.tile([P, BANK], F32, name="back", tag="back")
+                for b in range(4):
+                    m = 4 * h + b
+                    nc.tensor.transpose(turned[:, b * P : (b + 1) * P], olds[j][:, m * P : (m + 1) * P], identity[:])
+                for b in range(4):
+                    m = 4 * h + b
+                    nc.scalar.activation(
+                        scaled[:, b * P : (b + 1) * P],
+                        turned[:, b * P : (b + 1) * P],
+                        COPY,
+                        scale=retain_cols[:, m : m + 1],
+                    )
+                for b in range(4):
+                    nc.tensor.transpose(back[:, b * P : (b + 1) * P], scaled[:, b * P : (b + 1) * P], identity[:])
+                banks.append(back)
+            return banks
+
+        first, second, every = slice(0, HALF), slice(HALF, I), slice(0, I)
+
+        grouped0 = keep.tile([P, P, PACK], BF16, name="grouped0", align_bytes=64)
+        nc.scalar.copy(*interleaved(grouped0[:], raw0[:]))
+        nc.vector.tensor_copy(picked_planes[:], planes[:].indirect(gather_list[:]))
+        quantise(grouped0, slice(0, P))
+        nc.vector.tensor_copy(picked_words[:, first], words[:].indirect(gather_list[:, 0 : HALF // 16]))
+        nc.vector.tensor_copy(picked_words[:, second], words[:].indirect(gather_list[:, HALF // 16 : I // 16]))
+
+        v0a = keep.tile([P, HALF], F32, name="v0a")
+        project(0, first, v0a[:])
+        grouped1 = keep.tile([P, P, PACK], BF16, name="grouped1", align_bytes=64)
+        nc.scalar.copy(*interleaved(grouped1[:], raw1[:]))
+        v0b = keep.tile([P, HALF], F32, name="v0b", tag="stage1")
+        project(0, second, v0b[:])
+        grouped23 = keep.tile([P, 2 * P, PACK], BF16, name="grouped23", tag="late", align_bytes=64)
+        nc.scalar.copy(*interleaved(grouped23[:], raw23[:]))
+
+        scatter(0, first, v0a[:])
+        quantise(grouped1, slice(P, 2 * P))
+        scatter(0, second, v0b[:])
+        quantise(grouped23, slice(2 * P, 4 * P))
+
+        v1 = keep.tile([P, I], F32, name="v1", tag="stage23")
+        v2 = keep.tile([P, I], F32, name="v2")
+        v3 = keep.tile([P, I], F32, name="v3")
+        for j, v in ((1, v1), (2, v2), (3, v3)):
+            project(j, every, v[:])
+        for j, v in ((1, v1), (2, v2), (3, v3)):
+            scatter(j, every, v[:])
+
+        kept0 = keep.tile([P, T], F32, name="kept0", tag="late", align_bytes=64)
+        nc.gpsimd.tensor_tensor(kept0[:], olds[0][:], retain_wide[:], MULT)
+        nc.gpsimd.tensor_tensor(results[0][:], kept0[:], windows[0][:], ADD)
+        nc.sync.dma_start(out=out[0:P, :], in_=results[0][:])
+        for j in (1, 2):
+            kept = keep.tile([P, T], F32, name=f"kept{j}")
+            for h, bank in enumerate(scaled_old(j)):
+                nc.scalar.copy(kept[:, h * BANK : (h + 1) * BANK], bank[:])
+            nc.gpsimd.tensor_tensor(results[j][:], kept[:], windows[j][:], ADD)
+            nc.sync.dma_start(out=out[j * P : (j + 1) * P, :], in_=results[j][:])
+        last = E_TILES - 1
+        for h, bank in enumerate(scaled_old(last)):
+            cols = slice(h * BANK, (h + 1) * BANK)
+            nc.vector.tensor_tensor(results[last][:, cols], bank[:], windows[last][:, cols], ADD)
+            nc.sync.dma_start(out=out[last * P : (last + 1) * P, cols], in_=results[last][:, cols])

@@ -38,8 +38,7 @@ def tile_attend_cachewrite_kernel(tc, emb_words, emb_scales, wv, old, retain, of
 
     with ExitStack() as ctx:
         keep = ctx.enter_context(tc.tile_pool(name="keep", bufs=1))
-        v_psum = ctx.enter_context(tc.psum_pool(name="v_psum", bufs=2))
-        turn_psum = ctx.enter_context(tc.psum_pool(name="turn_psum", bufs=2))
+        psum = ctx.enter_context(tc.psum_pool(name="psum", bufs=1))
         back_psum = ctx.enter_context(tc.psum_pool(name="back_psum", bufs=4))
 
         gather_list = keep.tile([P, I // 16], U16, name="gather_list")
@@ -58,12 +57,12 @@ def tile_attend_cachewrite_kernel(tc, emb_words, emb_scales, wv, old, retain, of
         olds = [keep.tile([P, T], F32, name=f"old{j}") for j in range(E_TILES)]
         results = [keep.tile([P, T], F32, name=f"result{j}") for j in range(E_TILES)]
 
+        nc.vector.memset(retain_rows[:], 0.0)
         nc.vector.memset(planes[:].bitcast(I32), 0)
-        nc.gpsimd.memset(retain_rows[:], 0.0)
-        nc.sync.dma_start(out=retain_rows[0:T_BLOCKS, :], in_=retain.rearrange("o (m n) -> (o m) n", n=P))
-        nc.sync.dma_start(gather_list[:], offs)
         raw0 = keep.tile([P, PACK, P], F32, name="raw0")
         nc.sync.dma_start(out=raw0[:], in_=wv_rows[:, :, 0:P])
+        nc.sync.dma_start(out=retain_rows[0:T_BLOCKS, :], in_=retain.rearrange("o (m n) -> (o m) n", n=P))
+        nc.sync.dma_start(gather_list[:], offs)
         for q in range(4):
             nc.sync.dma_start(
                 out=planes[32 * q : 32 * q + 4, :].bitcast(I32),
@@ -85,11 +84,11 @@ def tile_attend_cachewrite_kernel(tc, emb_words, emb_scales, wv, old, retain, of
         for j in range(E_TILES):
             nc.vector.memset(windows[j][:], 0.0)
 
-        turned_rows = turn_psum.tile([P, BANK], F32, name="turned", tag="turned")
+        turned_rows = psum.tile([P, BANK], F32, name="turned_rows", tag="bank01")
         nc.tensor.transpose(turned_rows[:, 0:P], retain_rows[:], identity[:])
         nc.scalar.activation(retain_cols[:], turned_rows[:, 0:T_BLOCKS], COPY)
         for h in range(2):
-            spread = back_psum.tile([P, BANK], F32, name="back", tag="back")
+            spread = psum.tile([P, BANK], F32, name="spread", tag=f"bank1{h}")
             for b in range(4):
                 m = 4 * h + b
                 nc.tensor.transpose(
@@ -104,9 +103,9 @@ def tile_attend_cachewrite_kernel(tc, emb_words, emb_scales, wv, old, retain, of
                 in_=grouped[:].rearrange("p c r -> p (c r)"),
             )
 
-        def project(j, slots, dst):
+        def project(j, slots, dst, bank):
             n = slots.stop - slots.start
-            acc = v_psum.tile([P, BANK], F32, name="acc", tag="acc")
+            acc = psum.tile([P, BANK], F32, name="acc", tag=bank)
             nc.tensor.matmul_mx(
                 out=acc[:, 0:n],
                 lhsT=w_codes[:, j * P : (j + 1) * P].bitcast(FP8X4),
@@ -125,8 +124,8 @@ def tile_attend_cachewrite_kernel(tc, emb_words, emb_scales, wv, old, retain, of
         def scaled_old(j):
             banks = []
             for h in range(2):
-                turned = turn_psum.tile([P, BANK], F32, name="turned", tag="turned")
-                scaled = keep.tile([P, BANK], F32, name="scaled", tag="scaled", bufs=2)
+                turned = psum.tile([P, BANK], F32, name="turned", tag=f"bank{j % 2}{h}")
+                scaled = keep.tile([P, BANK], F32, name="scaled", tag="scaled", bufs=3)
                 back = back_psum.tile([P, BANK], F32, name="back", tag="back")
                 for b in range(4):
                     m = 4 * h + b
@@ -154,11 +153,11 @@ def tile_attend_cachewrite_kernel(tc, emb_words, emb_scales, wv, old, retain, of
         nc.vector.tensor_copy(picked_words[:, second], words[:].indirect(gather_list[:, HALF // 16 : I // 16]))
 
         v0a = keep.tile([P, HALF], F32, name="v0a")
-        project(0, first, v0a[:])
+        project(0, first, v0a[:], "bank10")
         grouped1 = keep.tile([P, P, PACK], BF16, name="grouped1", align_bytes=64)
         nc.scalar.copy(*interleaved(grouped1[:], raw1[:]))
         v0b = keep.tile([P, HALF], F32, name="v0b", tag="stage1")
-        project(0, second, v0b[:])
+        project(0, second, v0b[:], "bank11")
         grouped23 = keep.tile([P, 2 * P, PACK], BF16, name="grouped23", tag="late", align_bytes=64)
         nc.scalar.copy(*interleaved(grouped23[:], raw23[:]))
 
@@ -168,20 +167,20 @@ def tile_attend_cachewrite_kernel(tc, emb_words, emb_scales, wv, old, retain, of
         quantise(grouped23, slice(2 * P, 4 * P))
 
         v1 = keep.tile([P, I], F32, name="v1", tag="stage23")
-        v2 = keep.tile([P, I], F32, name="v2")
-        v3 = keep.tile([P, I], F32, name="v3")
-        for j, v in ((1, v1), (2, v2), (3, v3)):
-            project(j, every, v[:])
-        for j, v in ((1, v1), (2, v2), (3, v3)):
-            scatter(j, every, v[:])
+        project(1, every, v1[:], "bank00")
+        scatter(1, every, v1[:])
 
         kept0 = keep.tile([P, T], F32, name="kept0", tag="late", align_bytes=64)
         nc.gpsimd.tensor_tensor(kept0[:], olds[0][:], retain_wide[:], MULT)
         nc.gpsimd.tensor_tensor(results[0][:], kept0[:], windows[0][:], ADD)
         nc.sync.dma_start(out=out[0:P, :], in_=results[0][:])
         for j in (1, 2):
+            banks = scaled_old(j)
+            v = keep.tile([P, I], F32, name=f"v{j + 1}")
+            project(j + 1, every, v[:], f"bank{j % 2}0")
+            scatter(j + 1, every, v[:])
             kept = keep.tile([P, T], F32, name=f"kept{j}")
-            for h, bank in enumerate(scaled_old(j)):
+            for h, bank in enumerate(banks):
                 nc.scalar.copy(kept[:, h * BANK : (h + 1) * BANK], bank[:])
             nc.gpsimd.tensor_tensor(results[j][:], kept[:], windows[j][:], ADD)
             nc.sync.dma_start(out=out[j * P : (j + 1) * P, :], in_=results[j][:])

@@ -34,12 +34,10 @@ def interleaved(dst, src):
 
 def tile_attend_cachewrite_kernel(tc, emb_words, emb_scales, wv, old, retain, offs, offs2, out):
     nc = tc.nc
-    wv_rows = wv.rearrange("(p r) e -> p r e", r=PACK)
 
     with ExitStack() as ctx:
         keep = ctx.enter_context(tc.tile_pool(name="keep", bufs=1))
         psum = ctx.enter_context(tc.psum_pool(name="psum", bufs=1))
-        back_psum = ctx.enter_context(tc.psum_pool(name="back_psum", bufs=4))
 
         gather_list = keep.tile([P, I // 16], U16, name="gather_list")
         scatter_list = keep.tile([P, I // 16], U16, name="scatter_list")
@@ -53,48 +51,34 @@ def tile_attend_cachewrite_kernel(tc, emb_words, emb_scales, wv, old, retain, of
         retain_rows = keep.tile([P, P], F32, name="retain_rows")
         retain_cols = keep.tile([P, T_BLOCKS], F32, name="retain_cols")
         retain_wide = keep.tile([P, T], F32, name="retain_wide")
+        raw = keep.tile([P, PACK, E], F32, name="raw")
         windows = [keep.tile([P, T], F32, name=f"window{j}") for j in range(E_TILES)]
         olds = [keep.tile([P, T], F32, name=f"old{j}") for j in range(E_TILES)]
         results = [keep.tile([P, T], F32, name=f"result{j}") for j in range(E_TILES)]
 
-        nc.vector.memset(retain_rows[:], 0.0)
-        nc.vector.memset(planes[:].bitcast(I32), 0)
-        raw0 = keep.tile([P, PACK, P], F32, name="raw0")
-        nc.sync.dma_start(out=raw0[:], in_=wv_rows[:, :, 0:P])
-        nc.sync.dma_start(out=retain_rows[0:T_BLOCKS, :], in_=retain.rearrange("o (m n) -> (o m) n", n=P))
+        nc.gpsimd.memset(planes[:].bitcast(I32), 0)
+        nc.gpsimd.memset(retain_rows[:], 0.0)
+        make_identity(nc, identity[:])
+        for j in (0, 1):
+            nc.vector.memset(windows[j][:], 0.0)
+        for j in (2, 3):
+            nc.gpsimd.memset(windows[j][:], 0.0)
+
+        nc.sync.dma_start(out=raw[:], in_=wv.rearrange("(p r) e -> p r e", r=PACK))
         nc.sync.dma_start(gather_list[:], offs)
         for q in range(4):
             nc.sync.dma_start(
                 out=planes[32 * q : 32 * q + 4, :].bitcast(I32),
                 in_=emb_scales[0, 4 * q : 4 * q + 4, :].bitcast(I32),
             )
+        nc.sync.dma_start(out=retain_rows[0:T_BLOCKS, :], in_=retain.rearrange("o (m n) -> (o m) n", n=P))
         nc.sync.dma_start(
             out=words[:].bitcast(I32),
             in_=emb_words[0].rearrange("p c r -> p (c r)").bitcast(I32),
         )
         nc.sync.dma_start(scatter_list[:], offs2)
-        raw1 = keep.tile([P, PACK, P], F32, name="raw1", tag="stage1")
-        nc.sync.dma_start(out=raw1[:], in_=wv_rows[:, :, P : 2 * P])
-        raw23 = keep.tile([P, PACK, 2 * P], F32, name="raw23", tag="stage23")
-        nc.sync.dma_start(out=raw23[:], in_=wv_rows[:, :, 2 * P : 4 * P])
         for j in range(E_TILES):
             nc.sync.dma_start(out=olds[j][:], in_=old[j * P : (j + 1) * P, :])
-
-        make_identity(nc, identity[:])
-        for j in range(E_TILES):
-            nc.vector.memset(windows[j][:], 0.0)
-
-        turned_rows = psum.tile([P, BANK], F32, name="turned_rows", tag="bank01")
-        nc.tensor.transpose(turned_rows[:, 0:P], retain_rows[:], identity[:])
-        nc.scalar.activation(retain_cols[:], turned_rows[:, 0:T_BLOCKS], COPY)
-        for h in range(2):
-            spread = psum.tile([P, BANK], F32, name="spread", tag=f"bank1{h}")
-            for b in range(4):
-                m = 4 * h + b
-                nc.tensor.transpose(
-                    spread[:, b * P : (b + 1) * P], retain_cols[:, m : m + 1].to_broadcast([P, P]), identity[:]
-                )
-            nc.scalar.copy(retain_wide[:, h * BANK : (h + 1) * BANK], spread[:])
 
         def quantise(grouped, cols):
             nc.vector.quantize_mx(
@@ -103,7 +87,7 @@ def tile_attend_cachewrite_kernel(tc, emb_words, emb_scales, wv, old, retain, of
                 in_=grouped[:].rearrange("p c r -> p (c r)"),
             )
 
-        def project(j, slots, dst, bank):
+        def project(j, slots, bank):
             n = slots.stop - slots.start
             acc = psum.tile([P, BANK], F32, name="acc", tag=bank)
             nc.tensor.matmul_mx(
@@ -115,77 +99,100 @@ def tile_attend_cachewrite_kernel(tc, emb_words, emb_scales, wv, old, retain, of
                 start=True,
                 stop=True,
             )
-            nc.scalar.copy(dst, acc[:, 0:n])
+            return acc
 
-        def scatter(j, slots, src):
-            cols = slice(slots.start // 16, slots.stop // 16)
-            nc.vector.tensor_copy(windows[j][:].indirect(scatter_list[:, cols]), src)
-
-        def scaled_old(j):
-            banks = []
-            for h in range(2):
-                turned = psum.tile([P, BANK], F32, name="turned", tag=f"bank{j % 2}{h}")
-                scaled = keep.tile([P, BANK], F32, name="scaled", tag="scaled", bufs=3)
-                back = back_psum.tile([P, BANK], F32, name="back", tag="back")
-                for b in range(4):
-                    m = 4 * h + b
-                    nc.tensor.transpose(turned[:, b * P : (b + 1) * P], olds[j][:, m * P : (m + 1) * P], identity[:])
-                for b in range(4):
-                    m = 4 * h + b
-                    nc.scalar.activation(
-                        scaled[:, b * P : (b + 1) * P],
-                        turned[:, b * P : (b + 1) * P],
-                        COPY,
-                        scale=retain_cols[:, m : m + 1],
-                    )
-                for b in range(4):
-                    nc.tensor.transpose(back[:, b * P : (b + 1) * P], scaled[:, b * P : (b + 1) * P], identity[:])
-                banks.append(back)
-            return banks
+        def places(j, slots):
+            return windows[j][:].indirect(scatter_list[:, slots.start // 16 : slots.stop // 16])
 
         first, second, every = slice(0, HALF), slice(HALF, I), slice(0, I)
+        halves = (slice(0, BANK), slice(BANK, T))
 
-        grouped0 = keep.tile([P, P, PACK], BF16, name="grouped0", align_bytes=64)
-        nc.scalar.copy(*interleaved(grouped0[:], raw0[:]))
+        grouped01 = keep.tile([P, 2 * P, PACK], BF16, name="grouped01", align_bytes=64)
+        grouped23 = keep.tile([P, 2 * P, PACK], BF16, name="grouped23", align_bytes=64)
+        nc.scalar.copy(*interleaved(grouped23[:], raw[:, :, 2 * P : 4 * P]))
+        nc.vector.tensor_copy(*interleaved(grouped01[:], raw[:, :, 0 : 2 * P]))
         nc.vector.tensor_copy(picked_planes[:], planes[:].indirect(gather_list[:]))
-        quantise(grouped0, slice(0, P))
+        quantise(grouped01, slice(0, 2 * P))
+        quantise(grouped23, slice(2 * P, 4 * P))
+
+        turned_rows = psum.tile([P, BANK], F32, name="turned_rows", tag="p4")
+        nc.tensor.transpose(turned_rows[:, 0:P], retain_rows[:], identity[:])
+        nc.scalar.activation(retain_cols[:], turned_rows[:, 0:T_BLOCKS], COPY)
+        spread = []
+        for h in range(2):
+            bank = psum.tile([P, BANK], F32, name=f"spread{h}")
+            for b in range(4):
+                m = 4 * h + b
+                nc.tensor.transpose(
+                    bank[:, b * P : (b + 1) * P], retain_cols[:, m : m + 1].to_broadcast([P, P]), identity[:]
+                )
+            nc.scalar.copy(retain_wide[:, halves[h]], bank[:])
+            spread.append(bank)
+
         nc.vector.tensor_copy(picked_words[:, first], words[:].indirect(gather_list[:, 0 : HALF // 16]))
         nc.vector.tensor_copy(picked_words[:, second], words[:].indirect(gather_list[:, HALF // 16 : I // 16]))
 
         v0a = keep.tile([P, HALF], F32, name="v0a")
-        project(0, first, v0a[:], "bank10")
-        grouped1 = keep.tile([P, P, PACK], BF16, name="grouped1", align_bytes=64)
-        nc.scalar.copy(*interleaved(grouped1[:], raw1[:]))
-        v0b = keep.tile([P, HALF], F32, name="v0b", tag="stage1")
-        project(0, second, v0b[:], "bank11")
-        grouped23 = keep.tile([P, 2 * P, PACK], BF16, name="grouped23", tag="late", align_bytes=64)
-        nc.scalar.copy(*interleaved(grouped23[:], raw23[:]))
+        v0b = keep.tile([P, HALF], F32, name="v0b")
+        v1 = keep.tile([P, I], F32, name="v1", tag="after_scatter1")
+        v2 = keep.tile([P, I], F32, name="v2")
+        v3a = keep.tile([P, P], F32, name="v3a", tag="after_scatter3")
+        v3b = keep.tile([P, I - P], F32, name="v3b")
 
-        scatter(0, first, v0a[:])
-        quantise(grouped1, slice(P, 2 * P))
-        scatter(0, second, v0b[:])
-        quantise(grouped23, slice(2 * P, 4 * P))
+        nc.scalar.copy(v0a[:], project(0, first, "p0")[:, 0:HALF])
+        nc.vector.tensor_copy(v1[:, first], project(1, first, "p1")[:, 0:HALF])
+        nc.scalar.activation(places(0, first), v0a[:], COPY)
+        nc.vector.tensor_copy(v1[:, second], project(1, second, "p2")[:, 0:HALF])
+        nc.vector.tensor_copy(v0b[:], project(0, second, "p3")[:, 0:HALF])
+        nc.vector.tensor_copy(places(1, every), v1[:])
+        nc.scalar.activation(places(0, second), v0b[:], COPY)
+        nc.scalar.copy(v2[:], project(2, every, "p0")[:])
+        nc.scalar.activation(places(2, first), v2[:, first], COPY)
+        nc.scalar.activation(places(2, second), v2[:, second], COPY)
 
-        v1 = keep.tile([P, I], F32, name="v1", tag="stage23")
-        project(1, every, v1[:], "bank00")
-        scatter(1, every, v1[:])
-
-        kept0 = keep.tile([P, T], F32, name="kept0", tag="late", align_bytes=64)
+        kept0 = keep.tile([P, T], F32, name="kept0")
         nc.gpsimd.tensor_tensor(kept0[:], olds[0][:], retain_wide[:], MULT)
         nc.gpsimd.tensor_tensor(results[0][:], kept0[:], windows[0][:], ADD)
         nc.sync.dma_start(out=out[0:P, :], in_=results[0][:])
-        for j in (1, 2):
-            banks = scaled_old(j)
-            v = keep.tile([P, I], F32, name=f"v{j + 1}")
-            project(j + 1, every, v[:], f"bank{j % 2}0")
-            scatter(j + 1, every, v[:])
-            kept = keep.tile([P, T], F32, name=f"kept{j}")
-            for h, bank in enumerate(banks):
-                nc.scalar.copy(kept[:, h * BANK : (h + 1) * BANK], bank[:])
-            nc.gpsimd.tensor_tensor(results[j][:], kept[:], windows[j][:], ADD)
-            nc.sync.dma_start(out=out[j * P : (j + 1) * P, :], in_=results[j][:])
+
+        kept1 = keep.tile([P, T], F32, name="kept1", tag="after_scatter1")
+        for h in range(2):
+            nc.vector.tensor_tensor(kept1[:, halves[h]], olds[1][:, halves[h]], spread[h][:], MULT)
+        nc.gpsimd.tensor_tensor(results[1][:], kept1[:], windows[1][:], ADD)
+        nc.sync.dma_start(out=out[P : 2 * P, :], in_=results[1][:])
+
+        acc3 = project(3, every, "p1")
+        nc.vector.tensor_copy(v3a[:], acc3[:, 0:P])
+        nc.vector.tensor_copy(v3b[:], acc3[:, P:I])
+        nc.vector.tensor_copy(places(3, slice(0, P)), v3a[:])
+        nc.scalar.activation(places(3, slice(P, I)), v3b[:], COPY)
+
+        kept2 = keep.tile([P, T], F32, name="kept2", tag="after_scatter3")
+        for h in range(2):
+            nc.vector.tensor_tensor(kept2[:, halves[h]], olds[2][:, halves[h]], spread[h][:], MULT)
+        for h in range(2):
+            nc.gpsimd.tensor_tensor(results[2][:, halves[h]], kept2[:, halves[h]], windows[2][:, halves[h]], ADD)
+            nc.sync.dma_start(out=out[2 * P : 3 * P, halves[h]], in_=results[2][:, halves[h]])
+
         last = E_TILES - 1
-        for h, bank in enumerate(scaled_old(last)):
-            cols = slice(h * BANK, (h + 1) * BANK)
-            nc.vector.tensor_tensor(results[last][:, cols], bank[:], windows[last][:, cols], ADD)
-            nc.sync.dma_start(out=out[last * P : (last + 1) * P, cols], in_=results[last][:, cols])
+        backs = []
+        for h in range(2):
+            turned = psum.tile([P, BANK], F32, name="turned", tag=f"p{h}")
+            scaled = keep.tile([P, BANK], F32, name=f"scaled{h}")
+            back = psum.tile([P, BANK], F32, name="back", tag=f"p{4 + h}")
+            for b in range(4):
+                m = 4 * h + b
+                nc.tensor.transpose(turned[:, b * P : (b + 1) * P], olds[last][:, m * P : (m + 1) * P], identity[:])
+            for b in range(4):
+                m = 4 * h + b
+                nc.vector.tensor_scalar_mul(
+                    scaled[:, b * P : (b + 1) * P], turned[:, b * P : (b + 1) * P], retain_cols[:, m : m + 1]
+                )
+            for b in range(4):
+                nc.tensor.transpose(back[:, b * P : (b + 1) * P], scaled[:, b * P : (b + 1) * P], identity[:])
+            backs.append(back)
+        for c in range(4):
+            cols = slice(c * HALF, (c + 1) * HALF)
+            part = backs[c // 2][:, (c % 2) * HALF : (c % 2 + 1) * HALF]
+            nc.vector.tensor_tensor(results[last][:, cols], part, windows[last][:, cols], ADD)
+            nc.scalar.dma_start(out=out[last * P : (last + 1) * P, cols], in_=results[last][:, cols])

@@ -37,69 +37,70 @@ def tile_attend_cachewrite_kernel(tc, emb_words, emb_scales, wv, old, retain, of
 
     with ExitStack() as ctx:
         keep = ctx.enter_context(tc.tile_pool(name="keep", bufs=1))
+        late = ctx.enter_context(tc.tile_pool(name="late", bufs=1))
+        early = ctx.enter_context(tc.tile_pool(name="early", bufs=1))
         psum = ctx.enter_context(tc.psum_pool(name="psum", bufs=1))
 
         gather_list = keep.tile([P, I // 16], U16, name="gather_list")
         scatter_list = keep.tile([P, I // 16], U16, name="scatter_list")
-        words = keep.tile([P, U], U32, name="words", align_bytes=64)
-        planes = keep.tile([P, U], U8, name="planes", align_bytes=64)
-        picked_words = keep.tile([P, I], U32, name="picked_words", align_bytes=64)
-        picked_planes = keep.tile([P, I], U8, name="picked_planes", align_bytes=64)
-        w_codes = keep.tile([P, E], U32, name="w_codes", align_bytes=64)
+        words = late.tile([P, U], U32, name="words", offset=2048, align_bytes=64)
+        planes = keep.tile([P, U], U8, name="planes", tag="after_scale_gather", align_bytes=64)
         w_planes = keep.tile([P, E], U8, name="w_planes", align_bytes=64)
         identity = keep.tile([P, P], F32, name="identity")
-        retain_rows = keep.tile([P, P], F32, name="retain_rows")
-        retain_cols = keep.tile([P, T_BLOCKS], F32, name="retain_cols")
-        retain_wide = keep.tile([P, T], F32, name="retain_wide")
-        raw = keep.tile([P, PACK, E], F32, name="raw")
+        retain_cols = early.tile([P, 2, 4], F32, name="retain_cols", offset=0, align_bytes=64)
+        raw01 = keep.tile([P, PACK, 2 * P], F32, name="raw01")
+        raw23 = keep.tile([P, PACK, 2 * P], F32, name="raw23")
         windows = [keep.tile([P, T], F32, name=f"window{j}") for j in range(E_TILES)]
-        olds = [keep.tile([P, T], F32, name=f"old{j}") for j in range(E_TILES)]
-        results = [keep.tile([P, T], F32, name=f"result{j}") for j in range(E_TILES)]
+        olds = [
+            keep.tile([P, T], F32, name="old0"),
+            keep.tile([P, T], F32, name="old1", tag="old1"),
+            keep.tile([P, T], F32, name="old2", tag="after_product2"),
+            keep.tile([P, T], F32, name="old3", tag="after_product3"),
+        ]
 
-        nc.gpsimd.memset(planes[:].bitcast(I32), 0)
-        nc.gpsimd.memset(retain_rows[:], 0.0)
+        nc.vector.memset(planes[:].bitcast(I32), 0)
         make_identity(nc, identity[:])
-        for j in (0, 1):
-            nc.vector.memset(windows[j][:], 0.0)
-        for j in (2, 3):
-            nc.gpsimd.memset(windows[j][:], 0.0)
+        for window in windows[:2]:
+            nc.vector.memset(window[:], 0.0)
+        for window in windows[2:]:
+            nc.gpsimd.memset(window[:], 0.0)
 
-        nc.sync.dma_start(out=raw[:], in_=wv.rearrange("(p r) e -> p r e", r=PACK))
+        nc.sync.dma_start(out=retain_cols[:], in_=retain.rearrange("o (h p i) -> (o p) h i", h=2, i=4))
+        wv_rows = wv.rearrange("(p r) e -> p r e", r=PACK)
+        nc.sync.dma_start(out=raw01[:], in_=wv_rows[:, :, 0 : 2 * P])
         nc.sync.dma_start(gather_list[:], offs)
         for q in range(4):
             nc.sync.dma_start(
                 out=planes[32 * q : 32 * q + 4, :].bitcast(I32),
                 in_=emb_scales[0, 4 * q : 4 * q + 4, :].bitcast(I32),
             )
-        nc.sync.dma_start(out=retain_rows[0:T_BLOCKS, :], in_=retain.rearrange("o (m n) -> (o m) n", n=P))
         nc.sync.dma_start(
             out=words[:].bitcast(I32),
             in_=emb_words[0].rearrange("p c r -> p (c r)").bitcast(I32),
         )
+        nc.sync.dma_start(out=raw23[:], in_=wv_rows[:, :, 2 * P : 4 * P])
         nc.sync.dma_start(scatter_list[:], offs2)
-        for j in range(E_TILES):
+        for j in (1, 0, 2, 3):
             nc.sync.dma_start(out=olds[j][:], in_=old[j * P : (j + 1) * P, :])
 
-        def quantise(grouped, cols):
+        def quantise(grouped, half):
+            cols = slice(2 * P * half, 2 * P * (half + 1))
             nc.vector.quantize_mx(
-                out=w_codes[:, cols].bitcast(FP8X4),
+                out=w_codes[half][:].bitcast(FP8X4),
                 scales=w_planes[:, cols],
                 in_=grouped[:].rearrange("p c r -> p (c r)"),
             )
 
-        def project(j, slots, bank):
-            n = slots.stop - slots.start
-            acc = psum.tile([P, BANK], F32, name="acc", tag=bank)
+        def project(acc, j, slots):
             nc.tensor.matmul_mx(
-                out=acc[:, 0:n],
-                lhsT=w_codes[:, j * P : (j + 1) * P].bitcast(FP8X4),
+                out=acc[:, slots],
+                lhsT=w_codes[j // 2][:, (j % 2) * P : (j % 2 + 1) * P].bitcast(FP8X4),
                 lhsT_scale=w_planes[:, j * P : (j + 1) * P],
                 rhs=picked_words[:, slots].bitcast(FP8X4),
                 rhs_scale=picked_planes[:, slots],
                 start=True,
                 stop=True,
             )
-            return acc
 
         def places(j, slots):
             return windows[j][:].indirect(scatter_list[:, slots.start // 16 : slots.stop // 16])
@@ -107,92 +108,98 @@ def tile_attend_cachewrite_kernel(tc, emb_words, emb_scales, wv, old, retain, of
         first, second, every = slice(0, HALF), slice(HALF, I), slice(0, I)
         halves = (slice(0, BANK), slice(BANK, T))
 
-        grouped01 = keep.tile([P, 2 * P, PACK], BF16, name="grouped01", align_bytes=64)
-        grouped23 = keep.tile([P, 2 * P, PACK], BF16, name="grouped23", align_bytes=64)
-        nc.scalar.copy(*interleaved(grouped23[:], raw[:, :, 2 * P : 4 * P]))
-        nc.vector.tensor_copy(*interleaved(grouped01[:], raw[:, :, 0 : 2 * P]))
-        nc.vector.tensor_copy(picked_planes[:], planes[:].indirect(gather_list[:]))
-        quantise(grouped01, slice(0, 2 * P))
-        quantise(grouped23, slice(2 * P, 4 * P))
-
-        turned_rows = psum.tile([P, BANK], F32, name="turned_rows", tag="p4")
-        nc.tensor.transpose(turned_rows[:, 0:P], retain_rows[:], identity[:])
-        nc.scalar.activation(retain_cols[:], turned_rows[:, 0:T_BLOCKS], COPY)
         spread = []
         for h in range(2):
             bank = psum.tile([P, BANK], F32, name=f"spread{h}")
-            for b in range(4):
-                m = 4 * h + b
+            for i in range(4):
                 nc.tensor.transpose(
-                    bank[:, b * P : (b + 1) * P], retain_cols[:, m : m + 1].to_broadcast([P, P]), identity[:]
+                    bank[:].rearrange("q (p i) -> q i p", i=4)[:, i, :],
+                    retain_cols[:, h, i : i + 1].to_broadcast([P, P]),
+                    identity[:],
                 )
-            nc.scalar.copy(retain_wide[:, halves[h]], bank[:])
             spread.append(bank)
 
+        retain_wide = keep.tile([P, T], F32, name="retain_wide")
+        for h in range(2):
+            nc.scalar.copy(retain_wide[:, halves[h]], spread[h][:])
+        grouped01 = early.tile([P, 2 * P, PACK], BF16, name="grouped01", offset=64, align_bytes=64)
+        nc.vector.tensor_copy(*interleaved(grouped01[:], raw01[:]))
+        picked_planes = keep.tile([P, I], U8, name="picked_planes", align_bytes=64)
+        nc.vector.tensor_copy(picked_planes[:], planes[:].indirect(gather_list[:]))
+        w_codes = [
+            keep.tile([P, 2 * P], U32, name="codes01", tag="after_scale_gather", align_bytes=64),
+            keep.tile([P, 2 * P], U32, name="codes23", align_bytes=64),
+        ]
+        quantise(grouped01, 0)
+
+        picked_words = early.tile([P, I], U32, name="picked_words", offset=0, align_bytes=64)
         nc.vector.tensor_copy(picked_words[:, first], words[:].indirect(gather_list[:, 0 : HALF // 16]))
         nc.vector.tensor_copy(picked_words[:, second], words[:].indirect(gather_list[:, HALF // 16 : I // 16]))
 
-        v0a = keep.tile([P, HALF], F32, name="v0a")
-        v0b = keep.tile([P, HALF], F32, name="v0b")
-        v1 = keep.tile([P, I], F32, name="v1", tag="after_scatter1")
-        v2 = keep.tile([P, I], F32, name="v2")
-        v3a = keep.tile([P, P], F32, name="v3a", tag="after_scatter3")
-        v3b = keep.tile([P, I - P], F32, name="v3b")
+        split = 128
+        lead, rest = slice(0, split), slice(split, I)
+        v0a = late.tile([P, HALF], F32, name="v0a", offset=12288 + 512)
+        accs = [psum.tile([P, BANK], F32, name=f"acc{j}") for j in range(E_TILES)]
+        acc0b = psum.tile([P, BANK], F32, name="acc0b")
 
-        nc.scalar.copy(v0a[:], project(0, first, "p0")[:, 0:HALF])
-        nc.vector.tensor_copy(v1[:, first], project(1, first, "p1")[:, 0:HALF])
+        project(accs[0], 0, first)
+        nc.scalar.copy(v0a[:], accs[0][:, first])
         nc.scalar.activation(places(0, first), v0a[:], COPY)
-        nc.vector.tensor_copy(v1[:, second], project(1, second, "p2")[:, 0:HALF])
-        nc.vector.tensor_copy(v0b[:], project(0, second, "p3")[:, 0:HALF])
+        project(acc0b, 0, second)
+        project(accs[1], 1, every)
+        grouped23 = late.tile([P, 2 * P, PACK], BF16, name="grouped23", offset=5120, align_bytes=64)
+        nc.vector.tensor_copy(*interleaved(grouped23[:], raw23[:]))
+        v0b = keep.tile([P, HALF], F32, name="v0b")
+        nc.vector.tensor_copy(v0b[:], acc0b[:, second])
+        quantise(grouped23, 1)
+        project(accs[2], 2, every)
+        acc3a = psum.tile([P, BANK], F32, name="acc3a")
+        project(acc3a, 3, lead)
+        project(accs[3], 3, slice(split, HALF))
+        project(accs[3], 3, second)
+        v1 = late.tile([P, I], F32, name="v1", offset=6144)
+        nc.vector.tensor_copy(v1[:], accs[1][:])
         nc.vector.tensor_copy(places(1, every), v1[:])
+        v3a = late.tile([P, split], F32, name="v3a", offset=6144)
+        nc.vector.tensor_copy(v3a[:], acc3a[:, lead])
+        v2a = late.tile([P, HALF], F32, name="v2a", offset=12288)
+        v2b = late.tile([P, HALF], F32, name="v2b", offset=12288 + 1024)
+        nc.scalar.copy(v2a[:], accs[2][:, first])
         nc.scalar.activation(places(0, second), v0b[:], COPY)
-        nc.scalar.copy(v2[:], project(2, every, "p0")[:])
-        nc.scalar.activation(places(2, first), v2[:, first], COPY)
-        nc.scalar.activation(places(2, second), v2[:, second], COPY)
+        nc.scalar.copy(v2b[:], accs[2][:, second])
+        nc.scalar.activation(places(2, first), v2a[:], COPY)
+        v3b = late.tile([P, I - split], F32, name="v3b", offset=12288 - 512)
+        nc.scalar.copy(v3b[:], accs[3][:, rest])
+        nc.scalar.activation(places(2, second), v2b[:], COPY)
 
-        kept0 = keep.tile([P, T], F32, name="kept0")
-        nc.gpsimd.tensor_tensor(kept0[:], olds[0][:], retain_wide[:], MULT)
-        nc.gpsimd.tensor_tensor(results[0][:], kept0[:], windows[0][:], ADD)
+        def keep_old(j, kept, h):
+            nc.vector.tensor_tensor(kept[:, halves[h]], olds[j][:, halves[h]], spread[h][:], MULT)
+
+        results = [keep.tile([P, T], F32, name=f"result{j}") for j in range(2)]
+        kept01 = late.tile([P, T + BANK], F32, name="kept01", offset=0)
+        nc.gpsimd.tensor_tensor(kept01[:, T:], olds[1][:, halves[0]], retain_wide[:, halves[0]], MULT)
+        nc.gpsimd.tensor_tensor(kept01[:, 0:T], olds[0][:], retain_wide[:], MULT)
+        nc.gpsimd.tensor_tensor(results[0][:], kept01[:, 0:T], windows[0][:], ADD)
         nc.sync.dma_start(out=out[0:P, :], in_=results[0][:])
+        kept1b = late.tile([P, BANK], F32, name="kept1b", offset=7168)
+        nc.vector.tensor_tensor(kept1b[:], olds[1][:, halves[1]], spread[1][:], MULT)
+        nc.vector.tensor_copy(places(3, lead), v3a[:])
+        nc.scalar.activation(places(3, rest), v3b[:], COPY)
+        for cols, part in zip(halves, (kept01[:, T:], kept1b[:])):
+            nc.gpsimd.tensor_tensor(results[1][:, cols], part, windows[1][:, cols], ADD)
+            nc.sync.dma_start(out=out[P : 2 * P, cols], in_=results[1][:, cols])
 
-        kept1 = keep.tile([P, T], F32, name="kept1", tag="after_scatter1")
+        kept2 = keep.tile([P, T], F32, name="kept2", tag="old1")
         for h in range(2):
-            nc.vector.tensor_tensor(kept1[:, halves[h]], olds[1][:, halves[h]], spread[h][:], MULT)
-        nc.gpsimd.tensor_tensor(results[1][:], kept1[:], windows[1][:], ADD)
-        nc.sync.dma_start(out=out[P : 2 * P, :], in_=results[1][:])
-
-        acc3 = project(3, every, "p1")
-        nc.vector.tensor_copy(v3a[:], acc3[:, 0:P])
-        nc.vector.tensor_copy(v3b[:], acc3[:, P:I])
-        nc.vector.tensor_copy(places(3, slice(0, P)), v3a[:])
-        nc.scalar.activation(places(3, slice(P, I)), v3b[:], COPY)
-
-        kept2 = keep.tile([P, T], F32, name="kept2", tag="after_scatter3")
+            keep_old(2, kept2, h)
+        kept3 = keep.tile([P, T], F32, name="kept3", tag="after_product2")
         for h in range(2):
-            nc.vector.tensor_tensor(kept2[:, halves[h]], olds[2][:, halves[h]], spread[h][:], MULT)
-        for h in range(2):
-            nc.gpsimd.tensor_tensor(results[2][:, halves[h]], kept2[:, halves[h]], windows[2][:, halves[h]], ADD)
-            nc.sync.dma_start(out=out[2 * P : 3 * P, halves[h]], in_=results[2][:, halves[h]])
-
-        last = E_TILES - 1
-        backs = []
-        for h in range(2):
-            turned = psum.tile([P, BANK], F32, name="turned", tag=f"p{h}")
-            scaled = keep.tile([P, BANK], F32, name=f"scaled{h}")
-            back = psum.tile([P, BANK], F32, name="back", tag=f"p{4 + h}")
-            for b in range(4):
-                m = 4 * h + b
-                nc.tensor.transpose(turned[:, b * P : (b + 1) * P], olds[last][:, m * P : (m + 1) * P], identity[:])
-            for b in range(4):
-                m = 4 * h + b
-                nc.vector.tensor_scalar_mul(
-                    scaled[:, b * P : (b + 1) * P], turned[:, b * P : (b + 1) * P], retain_cols[:, m : m + 1]
-                )
-            for b in range(4):
-                nc.tensor.transpose(back[:, b * P : (b + 1) * P], scaled[:, b * P : (b + 1) * P], identity[:])
-            backs.append(back)
-        for c in range(4):
-            cols = slice(c * HALF, (c + 1) * HALF)
-            part = backs[c // 2][:, (c % 2) * HALF : (c % 2 + 1) * HALF]
-            nc.vector.tensor_tensor(results[last][:, cols], part, windows[last][:, cols], ADD)
-            nc.scalar.dma_start(out=out[last * P : (last + 1) * P, cols], in_=results[last][:, cols])
+            keep_old(3, kept3, h)
+        result2 = keep.tile([P, T], F32, name="result2", tag="after_product3")
+        for cols in halves:
+            nc.vector.tensor_tensor(result2[:, cols], kept2[:, cols], windows[2][:, cols], ADD)
+            nc.sync.dma_start(out=out[2 * P : 3 * P, cols], in_=result2[:, cols])
+        result3 = keep.tile([P, T], F32, name="result3", tag="old1")
+        for cols in (slice(0, HALF), slice(HALF, BANK + P), slice(BANK + P, T)):
+            nc.vector.tensor_tensor(result3[:, cols], kept3[:, cols], windows[3][:, cols], ADD)
+            nc.scalar.dma_start(out=out[3 * P : 4 * P, cols], in_=result3[:, cols])

@@ -47,17 +47,22 @@ def tile_attend_cachewrite_kernel(tc, emb_words, emb_scales, wv, old, retain, of
         planes = keep.tile([P, U], U8, name="planes", tag="after_scale_gather", align_bytes=64)
         w_planes = keep.tile([P, E], U8, name="w_planes", align_bytes=64)
         identity = keep.tile([P, P], F32, name="identity")
-        retain_cols = early.tile([P, 2, 4], F32, name="retain_cols", offset=0, align_bytes=64)
+        retain_rows = keep.tile([P, P], F32, name="retain_rows")
+        scale_cols = [
+            late.tile([P, 16], F32, name="scale_cols0", offset=16384),
+            keep.tile([P, 2], F32, name="scale_cols1"),
+        ]
         raw01 = keep.tile([P, PACK, 2 * P], F32, name="raw01")
         raw23 = keep.tile([P, PACK, 2 * P], F32, name="raw23")
-        windows = [keep.tile([P, T], F32, name=f"window{j}") for j in range(E_TILES)]
+        windows = [keep.tile([P, T], F32, name=f"window{j}", tag=f"window{j}") for j in range(E_TILES)]
         olds = [
             keep.tile([P, T], F32, name="old0"),
             keep.tile([P, T], F32, name="old1", tag="old1"),
             keep.tile([P, T], F32, name="old2", tag="after_product2"),
-            keep.tile([P, T], F32, name="old3", tag="after_product3"),
+            keep.tile([P, T], F32, name="old3"),
         ]
 
+        nc.vector.memset(retain_rows[:], 0.0)
         nc.vector.memset(planes[:].bitcast(I32), 0)
         make_identity(nc, identity[:])
         for window in windows[:2]:
@@ -65,9 +70,9 @@ def tile_attend_cachewrite_kernel(tc, emb_words, emb_scales, wv, old, retain, of
         for window in windows[2:]:
             nc.gpsimd.memset(window[:], 0.0)
 
-        nc.sync.dma_start(out=retain_cols[:], in_=retain.rearrange("o (h p i) -> (o p) h i", h=2, i=4))
         wv_rows = wv.rearrange("(p r) e -> p r e", r=PACK)
         nc.sync.dma_start(out=raw01[:], in_=wv_rows[:, :, 0 : 2 * P])
+        nc.sync.dma_start(out=retain_rows[0:T_BLOCKS, :], in_=retain.rearrange("o (m n) -> (o m) n", n=P))
         nc.sync.dma_start(gather_list[:], offs)
         for q in range(4):
             nc.sync.dma_start(
@@ -80,7 +85,7 @@ def tile_attend_cachewrite_kernel(tc, emb_words, emb_scales, wv, old, retain, of
         )
         nc.sync.dma_start(out=raw23[:], in_=wv_rows[:, :, 2 * P : 4 * P])
         nc.sync.dma_start(scatter_list[:], offs2)
-        for j in (1, 0, 2, 3):
+        for j in (1, 0, 3, 2):
             nc.sync.dma_start(out=olds[j][:], in_=old[j * P : (j + 1) * P, :])
 
         def quantise(grouped, half):
@@ -108,16 +113,22 @@ def tile_attend_cachewrite_kernel(tc, emb_words, emb_scales, wv, old, retain, of
         first, second, every = slice(0, HALF), slice(HALF, I), slice(0, I)
         halves = (slice(0, BANK), slice(BANK, T))
 
-        spread = []
-        for h in range(2):
-            bank = psum.tile([P, BANK], F32, name=f"spread{h}")
-            for i in range(4):
-                nc.tensor.transpose(
-                    bank[:].rearrange("q (p i) -> q i p", i=4)[:, i, :],
-                    retain_cols[:, h, i : i + 1].to_broadcast([P, P]),
-                    identity[:],
-                )
-            spread.append(bank)
+        def bank(name, number, count=1):
+            return psum.tile([P, count * BANK], F32, name=name, offset=number * BANK * 4)
+
+        turned_rows = bank("turned_rows", 2)
+        nc.tensor.transpose(turned_rows[:, 0:P], retain_rows[:], identity[:])
+        spread_cols = early.tile([P, T_BLOCKS], F32, name="spread_cols", offset=0, align_bytes=64)
+        nc.scalar.copy(spread_cols[:], turned_rows[:, 0:T_BLOCKS])
+        nc.scalar.copy(scale_cols[0][:, 0:6], turned_rows[:, 0:6])
+        nc.scalar.copy(scale_cols[1][:], turned_rows[:, 6:8])
+        spread = [bank(f"spread{h}", h) for h in range(2)]
+        for m in range(T_BLOCKS):
+            nc.tensor.transpose(
+                spread[m // 4][:, (m % 4) * P : (m % 4 + 1) * P],
+                spread_cols[:, m : m + 1].to_broadcast([P, P]),
+                identity[:],
+            )
 
         retain_wide = keep.tile([P, T], F32, name="retain_wide")
         for h in range(2):
@@ -136,11 +147,11 @@ def tile_attend_cachewrite_kernel(tc, emb_words, emb_scales, wv, old, retain, of
         nc.vector.tensor_copy(picked_words[:, first], words[:].indirect(gather_list[:, 0 : HALF // 16]))
         nc.vector.tensor_copy(picked_words[:, second], words[:].indirect(gather_list[:, HALF // 16 : I // 16]))
 
-        split = 128
+        split = HALF
         lead, rest = slice(0, split), slice(split, I)
-        v0a = late.tile([P, HALF], F32, name="v0a", offset=12288 + 512)
-        accs = [psum.tile([P, BANK], F32, name=f"acc{j}") for j in range(E_TILES)]
-        acc0b = psum.tile([P, BANK], F32, name="acc0b")
+        v0a = keep.tile([P, HALF], F32, name="v0a", tag="after_first_scatter")
+        accs = [bank(f"acc{j}", number) for j, number in enumerate((2, 4, 3, 6))]
+        acc0b = bank("acc0b", 5)
 
         project(accs[0], 0, first)
         nc.scalar.copy(v0a[:], accs[0][:, first])
@@ -152,25 +163,36 @@ def tile_attend_cachewrite_kernel(tc, emb_words, emb_scales, wv, old, retain, of
         v0b = keep.tile([P, HALF], F32, name="v0b")
         nc.vector.tensor_copy(v0b[:], acc0b[:, second])
         quantise(grouped23, 1)
-        project(accs[2], 2, every)
-        acc3a = psum.tile([P, BANK], F32, name="acc3a")
-        project(acc3a, 3, lead)
-        project(accs[3], 3, slice(split, HALF))
+        project(accs[2], 2, second)
+        acc3a = bank("acc3a", 7)
+        project(acc3a, 3, first)
+        acc2a = bank("acc2a", 2)
+        project(acc2a, 2, first)
         project(accs[3], 3, second)
         v1 = late.tile([P, I], F32, name="v1", offset=6144)
         nc.vector.tensor_copy(v1[:], accs[1][:])
-        nc.vector.tensor_copy(places(1, every), v1[:])
-        v3a = late.tile([P, split], F32, name="v3a", offset=6144)
+        v3a = keep.tile([P, split], F32, name="v3a", tag="after_lead")
         nc.vector.tensor_copy(v3a[:], acc3a[:, lead])
-        v2a = late.tile([P, HALF], F32, name="v2a", offset=12288)
-        v2b = late.tile([P, HALF], F32, name="v2b", offset=12288 + 1024)
-        nc.scalar.copy(v2a[:], accs[2][:, first])
-        nc.scalar.activation(places(0, second), v0b[:], COPY)
+        nc.vector.tensor_copy(places(1, every), v1[:])
+        nc.vector.tensor_copy(places(3, lead), v3a[:])
+        v2b = keep.tile([P, HALF], F32, name="v2b", tag="after_first_scatter")
         nc.scalar.copy(v2b[:], accs[2][:, second])
-        nc.scalar.activation(places(2, first), v2a[:], COPY)
-        v3b = late.tile([P, I - split], F32, name="v3b", offset=12288 - 512)
+        nc.scalar.activation(places(0, second), v0b[:], COPY)
+        turned = bank("turned", 4, 2)
+        scaled = keep.tile([P, T], F32, name="scaled")
+        blocks = [slice(m * P, (m + 1) * P) for m in range(T_BLOCKS)]
+        for block in blocks:
+            nc.tensor.transpose(turned[:, block], olds[3][:, block], identity[:])
+        for m, block in enumerate(blocks):
+            nc.scalar.activation(scaled[:, block], turned[:, block], COPY, scale=scale_cols[m // 6][:, m % 6 : m % 6 + 1])
+        v2a = late.tile([P, HALF], F32, name="v2a", offset=16384 + 32 - 1024)
+        v3b = late.tile([P, I - split], F32, name="v3b", offset=16384 + 32)
+        nc.scalar.copy(v2a[:], acc2a[:, first])
         nc.scalar.copy(v3b[:], accs[3][:, rest])
-        nc.scalar.activation(places(2, second), v2b[:], COPY)
+        back = bank("back", 2, 2)
+        for block in blocks:
+            nc.tensor.transpose(back[:, block], scaled[:, block], identity[:])
+        nc.scalar.activation(places(2, first), v2a[:], COPY)
 
         def keep_old(j, kept, h):
             nc.vector.tensor_tensor(kept[:, halves[h]], olds[j][:, halves[h]], spread[h][:], MULT)
@@ -183,8 +205,8 @@ def tile_attend_cachewrite_kernel(tc, emb_words, emb_scales, wv, old, retain, of
         nc.sync.dma_start(out=out[0:P, :], in_=results[0][:])
         kept1b = late.tile([P, BANK], F32, name="kept1b", offset=7168)
         nc.vector.tensor_tensor(kept1b[:], olds[1][:, halves[1]], spread[1][:], MULT)
-        nc.vector.tensor_copy(places(3, lead), v3a[:])
         nc.scalar.activation(places(3, rest), v3b[:], COPY)
+        nc.scalar.activation(places(2, second), v2b[:], COPY)
         for cols, part in zip(halves, (kept01[:, T:], kept1b[:])):
             nc.gpsimd.tensor_tensor(results[1][:, cols], part, windows[1][:, cols], ADD)
             nc.sync.dma_start(out=out[P : 2 * P, cols], in_=results[1][:, cols])
@@ -192,14 +214,11 @@ def tile_attend_cachewrite_kernel(tc, emb_words, emb_scales, wv, old, retain, of
         kept2 = keep.tile([P, T], F32, name="kept2", tag="old1")
         for h in range(2):
             keep_old(2, kept2, h)
-        kept3 = keep.tile([P, T], F32, name="kept3", tag="after_product2")
-        for h in range(2):
-            keep_old(3, kept3, h)
-        result2 = keep.tile([P, T], F32, name="result2", tag="after_product3")
+        result3 = keep.tile([P, T], F32, name="result3", tag="after_product2")
         for cols in halves:
-            nc.vector.tensor_tensor(result2[:, cols], kept2[:, cols], windows[2][:, cols], ADD)
-            nc.sync.dma_start(out=out[2 * P : 3 * P, cols], in_=result2[:, cols])
-        result3 = keep.tile([P, T], F32, name="result3", tag="old1")
+            nc.vector.tensor_tensor(result3[:, cols], back[:, cols], windows[3][:, cols], ADD)
+            nc.sync.dma_start(out=out[3 * P : 4 * P, cols], in_=result3[:, cols])
+        result2 = keep.tile([P, T], F32, name="result2", tag="window3")
         for cols in (slice(0, HALF), slice(HALF, BANK + P), slice(BANK + P, T)):
-            nc.vector.tensor_tensor(result3[:, cols], kept3[:, cols], windows[3][:, cols], ADD)
-            nc.scalar.dma_start(out=out[3 * P : 4 * P, cols], in_=result3[:, cols])
+            nc.vector.tensor_tensor(result2[:, cols], kept2[:, cols], windows[2][:, cols], ADD)
+            nc.scalar.dma_start(out=out[2 * P : 3 * P, cols], in_=result2[:, cols])

@@ -85,7 +85,7 @@ def tile_attend_cachewrite_kernel(tc, emb_words, emb_scales, wv, old, retain, of
         )
         nc.sync.dma_start(out=raw23[:], in_=wv_rows[:, :, 2 * P : 4 * P])
         nc.sync.dma_start(scatter_list[:], offs2)
-        for j in (1, 0, 3, 2):
+        for j in (0, 1, 3, 2):
             nc.sync.dma_start(out=olds[j][:], in_=old[j * P : (j + 1) * P, :])
 
         def quantise(grouped, half):
@@ -147,6 +147,9 @@ def tile_attend_cachewrite_kernel(tc, emb_words, emb_scales, wv, old, retain, of
         nc.vector.tensor_copy(picked_words[:, first], words[:].indirect(gather_list[:, 0 : HALF // 16]))
         nc.vector.tensor_copy(picked_words[:, second], words[:].indirect(gather_list[:, HALF // 16 : I // 16]))
 
+        def keep_old(j, kept, h):
+            nc.vector.tensor_tensor(kept, olds[j][:, halves[h]], spread[h][:], MULT)
+
         split = HALF
         lead, rest = slice(0, split), slice(split, I)
         v0a = keep.tile([P, HALF], F32, name="v0a", tag="after_first_scatter")
@@ -174,7 +177,11 @@ def tile_attend_cachewrite_kernel(tc, emb_words, emb_scales, wv, old, retain, of
         v3a = keep.tile([P, split], F32, name="v3a", tag="after_lead")
         nc.vector.tensor_copy(v3a[:], acc3a[:, lead])
         nc.vector.tensor_copy(places(1, every), v1[:])
+        kept1a = early.tile([P, BANK], F32, name="kept1a", offset=0)
+        keep_old(1, kept1a[:], 0)
         nc.vector.tensor_copy(places(3, lead), v3a[:])
+        kept1b = keep.tile([P, BANK], F32, name="kept1b", tag="after_lead")
+        keep_old(1, kept1b[:], 1)
         v2b = keep.tile([P, HALF], F32, name="v2b", tag="after_first_scatter")
         nc.scalar.copy(v2b[:], accs[2][:, second])
         nc.scalar.activation(places(0, second), v0b[:], COPY)
@@ -194,26 +201,20 @@ def tile_attend_cachewrite_kernel(tc, emb_words, emb_scales, wv, old, retain, of
             nc.tensor.transpose(back[:, block], scaled[:, block], identity[:])
         nc.scalar.activation(places(2, first), v2a[:], COPY)
 
-        def keep_old(j, kept, h):
-            nc.vector.tensor_tensor(kept[:, halves[h]], olds[j][:, halves[h]], spread[h][:], MULT)
-
         results = [keep.tile([P, T], F32, name=f"result{j}") for j in range(2)]
-        kept01 = late.tile([P, T + BANK], F32, name="kept01", offset=0)
-        nc.gpsimd.tensor_tensor(kept01[:, T:], olds[1][:, halves[0]], retain_wide[:, halves[0]], MULT)
-        nc.gpsimd.tensor_tensor(kept01[:, 0:T], olds[0][:], retain_wide[:], MULT)
-        nc.gpsimd.tensor_tensor(results[0][:], kept01[:, 0:T], windows[0][:], ADD)
+        kept0 = late.tile([P, T], F32, name="kept0", offset=2048)
+        nc.gpsimd.tensor_tensor(kept0[:], olds[0][:], retain_wide[:], MULT)
+        nc.gpsimd.tensor_tensor(results[0][:], kept0[:], windows[0][:], ADD)
         nc.sync.dma_start(out=out[0:P, :], in_=results[0][:])
-        kept1b = late.tile([P, BANK], F32, name="kept1b", offset=7168)
-        nc.vector.tensor_tensor(kept1b[:], olds[1][:, halves[1]], spread[1][:], MULT)
         nc.scalar.activation(places(3, rest), v3b[:], COPY)
         nc.scalar.activation(places(2, second), v2b[:], COPY)
-        for cols, part in zip(halves, (kept01[:, T:], kept1b[:])):
-            nc.gpsimd.tensor_tensor(results[1][:, cols], part, windows[1][:, cols], ADD)
+        for cols, kept1 in zip(halves, (kept1a, kept1b)):
+            nc.gpsimd.tensor_tensor(results[1][:, cols], kept1[:], windows[1][:, cols], ADD)
             nc.sync.dma_start(out=out[P : 2 * P, cols], in_=results[1][:, cols])
 
         kept2 = keep.tile([P, T], F32, name="kept2", tag="old1")
         for h in range(2):
-            keep_old(2, kept2, h)
+            keep_old(2, kept2[:, halves[h]], h)
         result3 = keep.tile([P, T], F32, name="result3", tag="after_product2")
         for cols in halves:
             nc.vector.tensor_tensor(result3[:, cols], back[:, cols], windows[3][:, cols], ADD)

@@ -58,8 +58,8 @@ def tile_attend_cachewrite_kernel(tc, emb_words, emb_scales, wv, old, retain, of
         olds = [
             keep.tile([P, T], F32, name="old0"),
             keep.tile([P, T], F32, name="old1", tag="old1"),
-            keep.tile([P, T], F32, name="old2", tag="after_product2"),
-            keep.tile([P, T], F32, name="old3"),
+            keep.tile([P, T], F32, name="old2"),
+            keep.tile([P, T], F32, name="old3", tag="after_product3"),
         ]
 
         nc.vector.memset(retain_rows[:], 0.0)
@@ -85,7 +85,7 @@ def tile_attend_cachewrite_kernel(tc, emb_words, emb_scales, wv, old, retain, of
         )
         nc.sync.dma_start(out=raw23[:], in_=wv_rows[:, :, 2 * P : 4 * P])
         nc.sync.dma_start(scatter_list[:], offs2)
-        for j in (0, 1, 3, 2):
+        for j in (0, 2, 1, 3):
             nc.sync.dma_start(out=olds[j][:], in_=old[j * P : (j + 1) * P, :])
 
         def quantise(grouped, half):
@@ -153,7 +153,7 @@ def tile_attend_cachewrite_kernel(tc, emb_words, emb_scales, wv, old, retain, of
         split = HALF
         lead, rest = slice(0, split), slice(split, I)
         v0a = keep.tile([P, HALF], F32, name="v0a", tag="after_first_scatter")
-        accs = [bank(f"acc{j}", number) for j, number in enumerate((2, 4, 3, 6))]
+        accs = [bank(f"acc{j}", number) for j, number in enumerate((2, 4, 3))]
         acc0b = bank("acc0b", 5)
 
         project(accs[0], 0, first)
@@ -166,60 +166,61 @@ def tile_attend_cachewrite_kernel(tc, emb_words, emb_scales, wv, old, retain, of
         v0b = keep.tile([P, HALF], F32, name="v0b")
         nc.vector.tensor_copy(v0b[:], acc0b[:, second])
         quantise(grouped23, 1)
-        project(accs[2], 2, second)
+        project(accs[2], 2, first)
         acc3a = bank("acc3a", 7)
         project(acc3a, 3, first)
-        acc2a = bank("acc2a", 2)
-        project(acc2a, 2, first)
-        project(accs[3], 3, second)
+        acc2b = bank("acc2b", 6)
+        project(acc2b, 2, second)
         v1 = late.tile([P, I], F32, name="v1", offset=6144)
         nc.vector.tensor_copy(v1[:], accs[1][:])
         v3a = keep.tile([P, split], F32, name="v3a", tag="after_lead")
         nc.vector.tensor_copy(v3a[:], acc3a[:, lead])
         nc.vector.tensor_copy(places(1, every), v1[:])
+        accs.append(bank("acc3b", 7))
+        project(accs[3], 3, second)
         kept1a = early.tile([P, BANK], F32, name="kept1a", offset=0)
         keep_old(1, kept1a[:], 0)
         nc.vector.tensor_copy(places(3, lead), v3a[:])
         kept1b = keep.tile([P, BANK], F32, name="kept1b", tag="after_lead")
         keep_old(1, kept1b[:], 1)
-        v2b = keep.tile([P, HALF], F32, name="v2b", tag="after_first_scatter")
-        nc.scalar.copy(v2b[:], accs[2][:, second])
+        v2a = keep.tile([P, HALF], F32, name="v2a", tag="after_first_scatter")
+        nc.scalar.copy(v2a[:], accs[2][:, first])
         nc.scalar.activation(places(0, second), v0b[:], COPY)
+        nc.scalar.activation(places(2, first), v2a[:], COPY)
         turned = bank("turned", 4, 2)
         scaled = keep.tile([P, T], F32, name="scaled")
         blocks = [slice(m * P, (m + 1) * P) for m in range(T_BLOCKS)]
         for block in blocks:
-            nc.tensor.transpose(turned[:, block], olds[3][:, block], identity[:])
+            nc.tensor.transpose(turned[:, block], olds[2][:, block], identity[:])
         for m, block in enumerate(blocks):
             nc.scalar.activation(scaled[:, block], turned[:, block], COPY, scale=scale_cols[m // 6][:, m % 6 : m % 6 + 1])
-        v2a = late.tile([P, HALF], F32, name="v2a", offset=16384 + 32 - 1024)
+        v2b = late.tile([P, HALF], F32, name="v2b", offset=16384 + 32 - 1024)
         v3b = late.tile([P, I - split], F32, name="v3b", offset=16384 + 32)
-        nc.scalar.copy(v2a[:], acc2a[:, first])
+        nc.scalar.copy(v2b[:], acc2b[:, second])
         nc.scalar.copy(v3b[:], accs[3][:, rest])
         back = bank("back", 2, 2)
         for block in blocks:
             nc.tensor.transpose(back[:, block], scaled[:, block], identity[:])
-        nc.scalar.activation(places(2, first), v2a[:], COPY)
+        nc.scalar.activation(places(2, second), v2b[:], COPY)
+        nc.scalar.activation(places(3, rest), v3b[:], COPY)
 
         results = [keep.tile([P, T], F32, name=f"result{j}") for j in range(2)]
         kept0 = late.tile([P, T], F32, name="kept0", offset=2048)
         nc.gpsimd.tensor_tensor(kept0[:], olds[0][:], retain_wide[:], MULT)
         nc.gpsimd.tensor_tensor(results[0][:], kept0[:], windows[0][:], ADD)
         nc.sync.dma_start(out=out[0:P, :], in_=results[0][:])
-        nc.scalar.activation(places(3, rest), v3b[:], COPY)
-        nc.scalar.activation(places(2, second), v2b[:], COPY)
         for cols, kept1 in zip(halves, (kept1a, kept1b)):
             nc.gpsimd.tensor_tensor(results[1][:, cols], kept1[:], windows[1][:, cols], ADD)
             nc.sync.dma_start(out=out[P : 2 * P, cols], in_=results[1][:, cols])
 
-        kept2 = keep.tile([P, T], F32, name="kept2", tag="old1")
+        kept3 = keep.tile([P, T], F32, name="kept3", tag="old1")
         for h in range(2):
-            keep_old(2, kept2[:, halves[h]], h)
-        result3 = keep.tile([P, T], F32, name="result3", tag="after_product2")
+            keep_old(3, kept3[:, halves[h]], h)
+        result2 = keep.tile([P, T], F32, name="result2", tag="after_product3")
         for cols in halves:
-            nc.vector.tensor_tensor(result3[:, cols], back[:, cols], windows[3][:, cols], ADD)
-            nc.sync.dma_start(out=out[3 * P : 4 * P, cols], in_=result3[:, cols])
-        result2 = keep.tile([P, T], F32, name="result2", tag="window3")
+            nc.vector.tensor_tensor(result2[:, cols], back[:, cols], windows[2][:, cols], ADD)
+            nc.sync.dma_start(out=out[2 * P : 3 * P, cols], in_=result2[:, cols])
+        result3 = keep.tile([P, T], F32, name="result3", tag="window2")
         for cols in (slice(0, HALF), slice(HALF, BANK + P), slice(BANK + P, T)):
-            nc.vector.tensor_tensor(result2[:, cols], kept2[:, cols], windows[2][:, cols], ADD)
-            nc.scalar.dma_start(out=out[2 * P : 3 * P, cols], in_=result2[:, cols])
+            nc.vector.tensor_tensor(result3[:, cols], kept3[:, cols], windows[3][:, cols], ADD)
+            nc.scalar.dma_start(out=out[3 * P : 4 * P, cols], in_=result3[:, cols])

@@ -218,7 +218,7 @@ def tile_attend_cachewrite_kernel(tc, emb_words, emb_scales, wv, old, retain, of
             keep_old(3, kept3[:, halves[h]], h)
         result2 = keep.tile([P, T], F32, name="result2", tag="after_product3")
         for cols in halves:
-            nc.vector.tensor_tensor(result2[:, cols], back[:, cols], windows[2][:, cols], ADD)
+            nc.vector.tensor_tensor(result2[:, cols], windows[2][:, cols], back[:, cols], ADD)
             nc.sync.dma_start(out=out[2 * P : 3 * P, cols], in_=result2[:, cols])
         result3 = keep.tile([P, T], F32, name="result3", tag="window2")
         for cols in (slice(0, HALF), slice(HALF, BANK + P), slice(BANK + P, T)):

@@ -38,7 +38,6 @@ def tile_attend_cachewrite_kernel(tc, emb_words, emb_scales, wv, old, retain, of
     with ExitStack() as ctx:
         keep = ctx.enter_context(tc.tile_pool(name="keep", bufs=1))
         late = ctx.enter_context(tc.tile_pool(name="late", bufs=1))
-        early = ctx.enter_context(tc.tile_pool(name="early", bufs=1))
         psum = ctx.enter_context(tc.psum_pool(name="psum", bufs=1))
 
         gather_list = keep.tile([P, I // 16], U16, name="gather_list")
@@ -47,12 +46,12 @@ def tile_attend_cachewrite_kernel(tc, emb_words, emb_scales, wv, old, retain, of
         planes = keep.tile([P, U], U8, name="planes", tag="after_scale_gather", align_bytes=64)
         w_planes = keep.tile([P, E], U8, name="w_planes", align_bytes=64)
         identity = keep.tile([P, P], F32, name="identity")
-        retain_rows = keep.tile([P, P], F32, name="retain_rows")
+        retain_rows = keep.tile([P, P], F32, name="retain_rows", tag="after_turn", align_bytes=64)
         scale_cols = [
             late.tile([P, 16], F32, name="scale_cols0", offset=16384),
             keep.tile([P, 2], F32, name="scale_cols1"),
         ]
-        raw01 = keep.tile([P, PACK, 2 * P], F32, name="raw01")
+        raw01 = keep.tile([P, PACK, 2 * P], F32, name="raw01", tag="after_interleave")
         raw23 = keep.tile([P, PACK, 2 * P], F32, name="raw23")
         windows = [keep.tile([P, T], F32, name=f"window{j}", tag=f"window{j}") for j in range(E_TILES)]
         olds = [
@@ -65,10 +64,8 @@ def tile_attend_cachewrite_kernel(tc, emb_words, emb_scales, wv, old, retain, of
         nc.vector.memset(retain_rows[:], 0.0)
         nc.vector.memset(planes[:].bitcast(I32), 0)
         make_identity(nc, identity[:])
-        for window in windows[:2]:
+        for window in windows:
             nc.vector.memset(window[:], 0.0)
-        for window in windows[2:]:
-            nc.gpsimd.memset(window[:], 0.0)
 
         wv_rows = wv.rearrange("(p r) e -> p r e", r=PACK)
         nc.sync.dma_start(out=raw01[:], in_=wv_rows[:, :, 0 : 2 * P])
@@ -118,7 +115,7 @@ def tile_attend_cachewrite_kernel(tc, emb_words, emb_scales, wv, old, retain, of
 
         turned_rows = bank("turned_rows", 2)
         nc.tensor.transpose(turned_rows[:, 0:P], retain_rows[:], identity[:])
-        spread_cols = early.tile([P, T_BLOCKS], F32, name="spread_cols", offset=0, align_bytes=64)
+        spread_cols = keep.tile([P, T_BLOCKS], F32, name="spread_cols")
         nc.scalar.copy(spread_cols[:], turned_rows[:, 0:T_BLOCKS])
         nc.scalar.copy(scale_cols[0][:, 0:6], turned_rows[:, 0:6])
         nc.scalar.copy(scale_cols[1][:], turned_rows[:, 6:8])
@@ -130,11 +127,11 @@ def tile_attend_cachewrite_kernel(tc, emb_words, emb_scales, wv, old, retain, of
                 identity[:],
             )
 
-        retain_wide = keep.tile([P, T], F32, name="retain_wide")
+        grouped01 = keep.tile([P, 2 * P, PACK], BF16, name="grouped01", tag="after_turn", align_bytes=64)
+        nc.scalar.copy(*interleaved(grouped01[:], raw01[:]))
+        retain_wide = keep.tile([P, T], F32, name="retain_wide", tag="after_interleave")
         for h in range(2):
             nc.scalar.copy(retain_wide[:, halves[h]], spread[h][:])
-        grouped01 = early.tile([P, 2 * P, PACK], BF16, name="grouped01", offset=64, align_bytes=64)
-        nc.vector.tensor_copy(*interleaved(grouped01[:], raw01[:]))
         picked_planes = keep.tile([P, I], U8, name="picked_planes", align_bytes=64)
         nc.vector.tensor_copy(picked_planes[:], planes[:].indirect(gather_list[:]))
         w_codes = [
@@ -143,7 +140,7 @@ def tile_attend_cachewrite_kernel(tc, emb_words, emb_scales, wv, old, retain, of
         ]
         quantise(grouped01, 0)
 
-        picked_words = early.tile([P, I], U32, name="picked_words", offset=0, align_bytes=64)
+        picked_words = keep.tile([P, I], U32, name="picked_words", tag="after_turn", align_bytes=64)
         nc.vector.tensor_copy(picked_words[:, first], words[:].indirect(gather_list[:, 0 : HALF // 16]))
         nc.vector.tensor_copy(picked_words[:, second], words[:].indirect(gather_list[:, HALF // 16 : I // 16]))
 
@@ -178,7 +175,7 @@ def tile_attend_cachewrite_kernel(tc, emb_words, emb_scales, wv, old, retain, of
         nc.vector.tensor_copy(places(1, every), v1[:])
         accs.append(bank("acc3b", 7))
         project(accs[3], 3, second)
-        kept1a = early.tile([P, BANK], F32, name="kept1a", offset=0)
+        kept1a = keep.tile([P, BANK], F32, name="kept1a", tag="after_turn", align_bytes=64)
         keep_old(1, kept1a[:], 0)
         nc.vector.tensor_copy(places(3, lead), v3a[:])
         kept1b = keep.tile([P, BANK], F32, name="kept1b", tag="after_lead")

@@ -38,6 +38,7 @@ def tile_attend_cachewrite_kernel(tc, emb_words, emb_scales, wv, old, retain, of
     with ExitStack() as ctx:
         keep = ctx.enter_context(tc.tile_pool(name="keep", bufs=1))
         late = ctx.enter_context(tc.tile_pool(name="late", bufs=1))
+        early = ctx.enter_context(tc.tile_pool(name="early", bufs=1))
         psum = ctx.enter_context(tc.psum_pool(name="psum", bufs=1))
 
         gather_list = keep.tile([P, I // 16], U16, name="gather_list")
@@ -46,14 +47,15 @@ def tile_attend_cachewrite_kernel(tc, emb_words, emb_scales, wv, old, retain, of
         planes = keep.tile([P, U], U8, name="planes", tag="after_scale_gather", align_bytes=64)
         w_planes = keep.tile([P, E], U8, name="w_planes", align_bytes=64)
         identity = keep.tile([P, P], F32, name="identity")
-        retain_rows = keep.tile([P, P], F32, name="retain_rows", tag="after_turn", align_bytes=64)
+        retain_rows = early.tile([P, P], F32, name="retain_rows", offset=2080)
         scale_cols = [
             late.tile([P, 16], F32, name="scale_cols0", offset=16384),
             keep.tile([P, 2], F32, name="scale_cols1"),
         ]
         raw01 = keep.tile([P, PACK, 2 * P], F32, name="raw01", tag="after_interleave")
         raw23 = keep.tile([P, PACK, 2 * P], F32, name="raw23")
-        windows = [keep.tile([P, T], F32, name=f"window{j}", tag=f"window{j}") for j in range(E_TILES)]
+        windows = [keep.tile([P, T], F32, name=f"window{j}", tag=f"window{j}") for j in range(E_TILES - 1)]
+        windows.append(windows[0])
         olds = [
             keep.tile([P, T], F32, name="old0"),
             keep.tile([P, T], F32, name="old1", tag="old1"),
@@ -64,8 +66,9 @@ def tile_attend_cachewrite_kernel(tc, emb_words, emb_scales, wv, old, retain, of
         nc.vector.memset(retain_rows[:], 0.0)
         nc.vector.memset(planes[:].bitcast(I32), 0)
         make_identity(nc, identity[:])
-        for window in windows:
-            nc.vector.memset(window[:], 0.0)
+        for window in windows[:2]:
+            nc.vector.memset(window[:].bitcast(I32), 0)
+        nc.gpsimd.memset(windows[2][:].bitcast(I32), 0)
 
         wv_rows = wv.rearrange("(p r) e -> p r e", r=PACK)
         nc.sync.dma_start(out=raw01[:], in_=wv_rows[:, :, 0 : 2 * P])
@@ -115,7 +118,7 @@ def tile_attend_cachewrite_kernel(tc, emb_words, emb_scales, wv, old, retain, of
 
         turned_rows = bank("turned_rows", 2)
         nc.tensor.transpose(turned_rows[:, 0:P], retain_rows[:], identity[:])
-        spread_cols = keep.tile([P, T_BLOCKS], F32, name="spread_cols")
+        spread_cols = early.tile([P, T_BLOCKS], F32, name="spread_cols", offset=0, align_bytes=64)
         nc.scalar.copy(spread_cols[:], turned_rows[:, 0:T_BLOCKS])
         nc.scalar.copy(scale_cols[0][:, 0:6], turned_rows[:, 0:6])
         nc.scalar.copy(scale_cols[1][:], turned_rows[:, 6:8])
@@ -127,7 +130,7 @@ def tile_attend_cachewrite_kernel(tc, emb_words, emb_scales, wv, old, retain, of
                 identity[:],
             )
 
-        grouped01 = keep.tile([P, 2 * P, PACK], BF16, name="grouped01", tag="after_turn", align_bytes=64)
+        grouped01 = early.tile([P, 2 * P, PACK], BF16, name="grouped01", offset=64, align_bytes=64)
         nc.scalar.copy(*interleaved(grouped01[:], raw01[:]))
         retain_wide = keep.tile([P, T], F32, name="retain_wide", tag="after_interleave")
         for h in range(2):
@@ -140,7 +143,7 @@ def tile_attend_cachewrite_kernel(tc, emb_words, emb_scales, wv, old, retain, of
         ]
         quantise(grouped01, 0)
 
-        picked_words = keep.tile([P, I], U32, name="picked_words", tag="after_turn", align_bytes=64)
+        picked_words = early.tile([P, I], U32, name="picked_words", offset=0, align_bytes=64)
         nc.vector.tensor_copy(picked_words[:, first], words[:].indirect(gather_list[:, 0 : HALF // 16]))
         nc.vector.tensor_copy(picked_words[:, second], words[:].indirect(gather_list[:, HALF // 16 : I // 16]))
 
@@ -175,11 +178,9 @@ def tile_attend_cachewrite_kernel(tc, emb_words, emb_scales, wv, old, retain, of
         nc.vector.tensor_copy(places(1, every), v1[:])
         accs.append(bank("acc3b", 7))
         project(accs[3], 3, second)
-        kept1a = keep.tile([P, BANK], F32, name="kept1a", tag="after_turn", align_bytes=64)
-        keep_old(1, kept1a[:], 0)
-        nc.vector.tensor_copy(places(3, lead), v3a[:])
-        kept1b = keep.tile([P, BANK], F32, name="kept1b", tag="after_lead")
-        keep_old(1, kept1b[:], 1)
+        kept1 = early.tile([P, T], F32, name="kept1", offset=0)
+        for h in range(2):
+            keep_old(1, kept1[:, halves[h]], h)
         v2a = keep.tile([P, HALF], F32, name="v2a", tag="after_first_scatter")
         nc.scalar.copy(v2a[:], accs[2][:, first])
         nc.scalar.activation(places(0, second), v0b[:], COPY)
@@ -199,25 +200,32 @@ def tile_attend_cachewrite_kernel(tc, emb_words, emb_scales, wv, old, retain, of
         for block in blocks:
             nc.tensor.transpose(back[:, block], scaled[:, block], identity[:])
         nc.scalar.activation(places(2, second), v2b[:], COPY)
-        nc.scalar.activation(places(3, rest), v3b[:], COPY)
 
         results = [keep.tile([P, T], F32, name=f"result{j}") for j in range(2)]
         kept0 = late.tile([P, T], F32, name="kept0", offset=2048)
         nc.gpsimd.tensor_tensor(kept0[:], olds[0][:], retain_wide[:], MULT)
         nc.gpsimd.tensor_tensor(results[0][:], kept0[:], windows[0][:], ADD)
         nc.sync.dma_start(out=out[0:P, :], in_=results[0][:])
-        for cols, kept1 in zip(halves, (kept1a, kept1b)):
-            nc.gpsimd.tensor_tensor(results[1][:, cols], kept1[:], windows[1][:, cols], ADD)
+        for cols in halves:
+            nc.gpsimd.tensor_tensor(results[1][:, cols], kept1[:, cols], windows[1][:, cols], ADD)
             nc.sync.dma_start(out=out[P : 2 * P, cols], in_=results[1][:, cols])
 
-        kept3 = keep.tile([P, T], F32, name="kept3", tag="old1")
-        for h in range(2):
-            keep_old(3, kept3[:, halves[h]], h)
+        kept3a = keep.tile([P, BANK], F32, name="kept3a", tag="old1")
+        keep_old(3, kept3a[:], 0)
+        nc.vector.tensor_copy(places(3, lead), v3a[:])
+        nc.scalar.activation(places(3, rest), v3b[:], COPY)
+        kept3b = keep.tile([P, BANK], F32, name="kept3b", tag="after_lead")
+        keep_old(3, kept3b[:], 1)
         result2 = keep.tile([P, T], F32, name="result2", tag="after_product3")
         for cols in halves:
             nc.vector.tensor_tensor(result2[:, cols], windows[2][:, cols], back[:, cols], ADD)
             nc.sync.dma_start(out=out[2 * P : 3 * P, cols], in_=result2[:, cols])
         result3 = keep.tile([P, T], F32, name="result3", tag="window2")
-        for cols in (slice(0, HALF), slice(HALF, BANK + P), slice(BANK + P, T)):
-            nc.vector.tensor_tensor(result3[:, cols], kept3[:, cols], windows[3][:, cols], ADD)
+        pieces = (
+            (halves[0], kept3a[:]),
+            (slice(BANK, BANK + HALF), kept3b[:, 0:HALF]),
+            (slice(BANK + HALF, T), kept3b[:, HALF:BANK]),
+        )
+        for cols, kept3 in pieces:
+            nc.vector.tensor_tensor(result3[:, cols], kept3, windows[3][:, cols], ADD)
             nc.scalar.dma_start(out=out[3 * P : 4 * P, cols], in_=result3[:, cols])

@@ -66,9 +66,8 @@ def tile_attend_cachewrite_kernel(tc, emb_words, emb_scales, wv, old, retain, of
         nc.vector.memset(retain_rows[:], 0.0)
         nc.vector.memset(planes[:].bitcast(I32), 0)
         make_identity(nc, identity[:])
-        for window in windows[:2]:
+        for window in windows[:3]:
             nc.vector.memset(window[:].bitcast(I32), 0)
-        nc.gpsimd.memset(windows[2][:].bitcast(I32), 0)
 
         wv_rows = wv.rearrange("(p r) e -> p r e", r=PACK)
         nc.sync.dma_start(out=raw01[:], in_=wv_rows[:, :, 0 : 2 * P])
@@ -118,7 +117,7 @@ def tile_attend_cachewrite_kernel(tc, emb_words, emb_scales, wv, old, retain, of
 
         turned_rows = bank("turned_rows", 2)
         nc.tensor.transpose(turned_rows[:, 0:P], retain_rows[:], identity[:])
-        spread_cols = early.tile([P, T_BLOCKS], F32, name="spread_cols", offset=0, align_bytes=64)
+        spread_cols = keep.tile([P, T_BLOCKS], F32, name="spread_cols")
         nc.scalar.copy(spread_cols[:], turned_rows[:, 0:T_BLOCKS])
         nc.scalar.copy(scale_cols[0][:, 0:6], turned_rows[:, 0:6])
         nc.scalar.copy(scale_cols[1][:], turned_rows[:, 6:8])
@@ -131,7 +130,8 @@ def tile_attend_cachewrite_kernel(tc, emb_words, emb_scales, wv, old, retain, of
             )
 
         grouped01 = early.tile([P, 2 * P, PACK], BF16, name="grouped01", offset=64, align_bytes=64)
-        nc.scalar.copy(*interleaved(grouped01[:], raw01[:]))
+        nc.scalar.copy(*interleaved(grouped01[:, P : 2 * P, :], raw01[:, :, P : 2 * P]))
+        nc.vector.tensor_copy(*interleaved(grouped01[:, 0:P, :], raw01[:, :, 0:P]))
         retain_wide = keep.tile([P, T], F32, name="retain_wide", tag="after_interleave")
         for h in range(2):
             nc.scalar.copy(retain_wide[:, halves[h]], spread[h][:])

@@ -73,10 +73,10 @@ def tile_attend_cachewrite_kernel(tc, emb_words, emb_scales, wv, old, retain, of
         nc.sync.dma_start(out=raw01[:], in_=wv_rows[:, :, 0 : 2 * P])
         nc.sync.dma_start(out=retain_rows[0:T_BLOCKS, :], in_=retain.rearrange("o (m n) -> (o m) n", n=P))
         nc.sync.dma_start(gather_list[:], offs)
-        for q in range(4):
+        for r in range(4):
             nc.sync.dma_start(
-                out=planes[32 * q : 32 * q + 4, :].bitcast(I32),
-                in_=emb_scales[0, 4 * q : 4 * q + 4, :].bitcast(I32),
+                out=planes[r:P:32, :].bitcast(I32),
+                in_=emb_scales[0, r:16:4, :].bitcast(I32),
             )
         nc.sync.dma_start(
             out=words[:].bitcast(I32),
@@ -152,23 +152,27 @@ def tile_attend_cachewrite_kernel(tc, emb_words, emb_scales, wv, old, retain, of
 
         split = HALF
         lead, rest = slice(0, split), slice(split, I)
-        v0a = keep.tile([P, HALF], F32, name="v0a", tag="after_first_scatter")
-        accs = [bank(f"acc{j}", number) for j, number in enumerate((2, 4, 3))]
+        v0a = keep.tile([P, P], F32, name="v0a", tag="after_first_scatter")
+        v0b = keep.tile([P, I - P], F32, name="v0b")
+        accs = [bank(f"acc{j}", number) for j, number in enumerate((2, 4))]
         acc0b = bank("acc0b", 5)
 
-        project(accs[0], 0, first)
-        nc.scalar.copy(v0a[:], accs[0][:, first])
-        nc.scalar.activation(places(0, first), v0a[:], COPY)
+        acc0a = bank("acc0a", 3)
+        project(accs[0], 0, slice(0, P))
+        project(acc0a, 0, slice(P, HALF))
+        nc.scalar.copy(v0a[:], accs[0][:, 0:P])
+        nc.scalar.activation(places(0, slice(0, P)), v0a[:], COPY)
+        nc.scalar.copy(v0b[:, 0:P], acc0a[:, P:HALF])
         project(acc0b, 0, second)
         project(accs[1], 1, every)
         grouped23 = late.tile([P, 2 * P, PACK], BF16, name="grouped23", offset=5120, align_bytes=64)
         nc.vector.tensor_copy(*interleaved(grouped23[:], raw23[:]))
-        v0b = keep.tile([P, HALF], F32, name="v0b")
-        nc.vector.tensor_copy(v0b[:], acc0b[:, second])
+        nc.vector.tensor_copy(v0b[:, P:], acc0b[:, second])
         quantise(grouped23, 1)
-        project(accs[2], 2, first)
         acc3a = bank("acc3a", 7)
         project(acc3a, 3, first)
+        accs.append(bank("acc2a", 3))
+        project(accs[2], 2, first)
         acc2b = bank("acc2b", 6)
         project(acc2b, 2, second)
         v1 = late.tile([P, I], F32, name="v1", offset=6144)
@@ -182,8 +186,8 @@ def tile_attend_cachewrite_kernel(tc, emb_words, emb_scales, wv, old, retain, of
         for h in range(2):
             keep_old(1, kept1[:, halves[h]], h)
         v2a = keep.tile([P, HALF], F32, name="v2a", tag="after_first_scatter")
+        nc.scalar.activation(places(0, slice(P, I)), v0b[:], COPY)
         nc.scalar.copy(v2a[:], accs[2][:, first])
-        nc.scalar.activation(places(0, second), v0b[:], COPY)
         nc.scalar.activation(places(2, first), v2a[:], COPY)
         turned = bank("turned", 4, 2)
         scaled = keep.tile([P, T], F32, name="scaled")

@@ -54,8 +54,7 @@ def tile_attend_cachewrite_kernel(tc, emb_words, emb_scales, wv, old, retain, of
         ]
         raw01 = keep.tile([P, PACK, 2 * P], F32, name="raw01", tag="after_interleave")
         raw23 = keep.tile([P, PACK, 2 * P], F32, name="raw23")
-        windows = [keep.tile([P, T], F32, name=f"window{j}", tag=f"window{j}") for j in range(E_TILES - 1)]
-        windows.append(windows[0])
+        windows = [keep.tile([P, T], F32, name=f"window{j}", tag=f"window{j}") for j in range(E_TILES)]
         olds = [
             keep.tile([P, T], F32, name="old0"),
             keep.tile([P, T], F32, name="old1", tag="old1"),
@@ -66,7 +65,7 @@ def tile_attend_cachewrite_kernel(tc, emb_words, emb_scales, wv, old, retain, of
         nc.vector.memset(retain_rows[:], 0.0)
         nc.vector.memset(planes[:].bitcast(I32), 0)
         make_identity(nc, identity[:])
-        for window in windows[:3]:
+        for window in windows:
             nc.vector.memset(window[:].bitcast(I32), 0)
 
         wv_rows = wv.rearrange("(p r) e -> p r e", r=PACK)
@@ -84,13 +83,12 @@ def tile_attend_cachewrite_kernel(tc, emb_words, emb_scales, wv, old, retain, of
         )
         nc.sync.dma_start(out=raw23[:], in_=wv_rows[:, :, 2 * P : 4 * P])
         nc.sync.dma_start(scatter_list[:], offs2)
-        for j in (0, 2, 1, 3):
+        for j in range(E_TILES):
             nc.sync.dma_start(out=olds[j][:], in_=old[j * P : (j + 1) * P, :])
 
-        def quantise(grouped, half):
-            cols = slice(2 * P * half, 2 * P * (half + 1))
+        def quantise(grouped, codes, cols):
             nc.vector.quantize_mx(
-                out=w_codes[half][:].bitcast(FP8X4),
+                out=codes.bitcast(FP8X4),
                 scales=w_planes[:, cols],
                 in_=grouped[:].rearrange("p c r -> p (c r)"),
             )
@@ -129,9 +127,10 @@ def tile_attend_cachewrite_kernel(tc, emb_words, emb_scales, wv, old, retain, of
                 identity[:],
             )
 
-        grouped01 = early.tile([P, 2 * P, PACK], BF16, name="grouped01", offset=64, align_bytes=64)
-        nc.scalar.copy(*interleaved(grouped01[:, P : 2 * P, :], raw01[:, :, P : 2 * P]))
-        nc.vector.tensor_copy(*interleaved(grouped01[:, 0:P, :], raw01[:, :, 0:P]))
+        grouped0 = early.tile([P, P, PACK], BF16, name="grouped0", offset=0, align_bytes=64)
+        grouped1 = early.tile([P, P, PACK], BF16, name="grouped1", offset=1088, align_bytes=64)
+        nc.scalar.copy(*interleaved(grouped1[:], raw01[:, :, P : 2 * P]))
+        nc.vector.tensor_copy(*interleaved(grouped0[:], raw01[:, :, 0:P]))
         retain_wide = keep.tile([P, T], F32, name="retain_wide", tag="after_interleave")
         for h in range(2):
             nc.scalar.copy(retain_wide[:, halves[h]], spread[h][:])
@@ -141,7 +140,8 @@ def tile_attend_cachewrite_kernel(tc, emb_words, emb_scales, wv, old, retain, of
             keep.tile([P, 2 * P], U32, name="codes01", tag="after_scale_gather", align_bytes=64),
             keep.tile([P, 2 * P], U32, name="codes23", align_bytes=64),
         ]
-        quantise(grouped01, 0)
+        quantise(grouped0, w_codes[0][:, 0:P], slice(0, P))
+        quantise(grouped1, w_codes[0][:, P : 2 * P], slice(P, 2 * P))
 
         picked_words = early.tile([P, I], U32, name="picked_words", offset=0, align_bytes=64)
         nc.vector.tensor_copy(picked_words[:, first], words[:].indirect(gather_list[:, 0 : HALF // 16]))
@@ -150,7 +150,7 @@ def tile_attend_cachewrite_kernel(tc, emb_words, emb_scales, wv, old, retain, of
         def keep_old(j, kept, h):
             nc.vector.tensor_tensor(kept, olds[j][:, halves[h]], spread[h][:], MULT)
 
-        split = HALF
+        split = 288
         lead, rest = slice(0, split), slice(split, I)
         v0a = keep.tile([P, P], F32, name="v0a", tag="after_first_scatter")
         v0b = keep.tile([P, I - P], F32, name="v0b")
@@ -160,31 +160,28 @@ def tile_attend_cachewrite_kernel(tc, emb_words, emb_scales, wv, old, retain, of
         acc0a = bank("acc0a", 3)
         project(accs[0], 0, slice(0, P))
         project(acc0a, 0, slice(P, HALF))
+        project(accs[1], 1, first)
         nc.scalar.copy(v0a[:], accs[0][:, 0:P])
         nc.scalar.activation(places(0, slice(0, P)), v0a[:], COPY)
         nc.scalar.copy(v0b[:, 0:P], acc0a[:, P:HALF])
         project(acc0b, 0, second)
-        project(accs[1], 1, every)
+        project(accs[1], 1, second)
         grouped23 = late.tile([P, 2 * P, PACK], BF16, name="grouped23", offset=5120, align_bytes=64)
         nc.vector.tensor_copy(*interleaved(grouped23[:], raw23[:]))
         nc.vector.tensor_copy(v0b[:, P:], acc0b[:, second])
-        quantise(grouped23, 1)
-        acc3a = bank("acc3a", 7)
-        project(acc3a, 3, first)
-        accs.append(bank("acc2a", 3))
-        project(accs[2], 2, first)
-        acc2b = bank("acc2b", 6)
-        project(acc2b, 2, second)
-        v1 = late.tile([P, I], F32, name="v1", offset=6144)
+        v1 = keep.tile([P, I], F32, name="v1")
         nc.vector.tensor_copy(v1[:], accs[1][:])
-        v3a = keep.tile([P, split], F32, name="v3a", tag="after_lead")
-        nc.vector.tensor_copy(v3a[:], acc3a[:, lead])
+        quantise(grouped23, w_codes[1][:], slice(2 * P, 4 * P))
         nc.vector.tensor_copy(places(1, every), v1[:])
-        accs.append(bank("acc3b", 7))
-        project(accs[3], 3, second)
+        accs.extend([bank("acc2", 6), bank("acc3", 7)])
+        project(accs[2], 2, every)
+        project(accs[3], 3, every)
+        v3a = keep.tile([P, split], F32, name="v3a", tag="after_lead")
+        nc.vector.tensor_copy(v3a[:], accs[3][:, lead])
         kept1 = early.tile([P, T], F32, name="kept1", offset=0)
         for h in range(2):
             keep_old(1, kept1[:, halves[h]], h)
+        nc.vector.tensor_copy(places(3, lead), v3a[:])
         v2a = keep.tile([P, HALF], F32, name="v2a", tag="after_first_scatter")
         nc.scalar.activation(places(0, slice(P, I)), v0b[:], COPY)
         nc.scalar.copy(v2a[:], accs[2][:, first])
@@ -198,7 +195,7 @@ def tile_attend_cachewrite_kernel(tc, emb_words, emb_scales, wv, old, retain, of
             nc.scalar.activation(scaled[:, block], turned[:, block], COPY, scale=scale_cols[m // 6][:, m % 6 : m % 6 + 1])
         v2b = late.tile([P, HALF], F32, name="v2b", offset=16384 + 32 - 1024)
         v3b = late.tile([P, I - split], F32, name="v3b", offset=16384 + 32)
-        nc.scalar.copy(v2b[:], acc2b[:, second])
+        nc.scalar.copy(v2b[:], accs[2][:, second])
         nc.scalar.copy(v3b[:], accs[3][:, rest])
         back = bank("back", 2, 2)
         for block in blocks:
@@ -214,10 +211,9 @@ def tile_attend_cachewrite_kernel(tc, emb_words, emb_scales, wv, old, retain, of
             nc.gpsimd.tensor_tensor(results[1][:, cols], kept1[:, cols], windows[1][:, cols], ADD)
             nc.sync.dma_start(out=out[P : 2 * P, cols], in_=results[1][:, cols])
 
+        nc.scalar.activation(places(3, rest), v3b[:], COPY)
         kept3a = keep.tile([P, BANK], F32, name="kept3a", tag="old1")
         keep_old(3, kept3a[:], 0)
-        nc.vector.tensor_copy(places(3, lead), v3a[:])
-        nc.scalar.activation(places(3, rest), v3b[:], COPY)
         kept3b = keep.tile([P, BANK], F32, name="kept3b", tag="after_lead")
         keep_old(3, kept3b[:], 1)
         result2 = keep.tile([P, T], F32, name="result2", tag="after_product3")

@@ -57,9 +57,9 @@ def tile_attend_cachewrite_kernel(tc, emb_words, emb_scales, wv, old, retain, of
         windows = [keep.tile([P, T], F32, name=f"window{j}", tag=f"window{j}") for j in range(E_TILES)]
         olds = [
             keep.tile([P, T], F32, name="old0"),
-            keep.tile([P, T], F32, name="old1", tag="old1"),
+            keep.tile([P, T], F32, name="old1"),
             keep.tile([P, T], F32, name="old2"),
-            keep.tile([P, T], F32, name="old3", tag="after_product3"),
+            keep.tile([P, T], F32, name="old3"),
         ]
 
         nc.vector.memset(retain_rows[:], 0.0)
@@ -152,42 +152,40 @@ def tile_attend_cachewrite_kernel(tc, emb_words, emb_scales, wv, old, retain, of
 
         split = 288
         lead, rest = slice(0, split), slice(split, I)
-        v0a = keep.tile([P, P], F32, name="v0a", tag="after_first_scatter")
-        v0b = keep.tile([P, I - P], F32, name="v0b")
+        v0a = keep.tile([P, HALF], F32, name="v0a")
+        v0b = keep.tile([P, HALF], F32, name="v0b")
         accs = [bank(f"acc{j}", number) for j, number in enumerate((2, 4))]
         acc0b = bank("acc0b", 5)
 
-        acc0a = bank("acc0a", 3)
-        project(accs[0], 0, slice(0, P))
-        project(acc0a, 0, slice(P, HALF))
+        project(accs[0], 0, first)
         project(accs[1], 1, first)
-        nc.scalar.copy(v0a[:], accs[0][:, 0:P])
-        nc.scalar.activation(places(0, slice(0, P)), v0a[:], COPY)
-        nc.scalar.copy(v0b[:, 0:P], acc0a[:, P:HALF])
-        project(acc0b, 0, second)
+        nc.scalar.copy(v0a[:], accs[0][:, first])
+        nc.scalar.activation(places(0, first), v0a[:], COPY)
         project(accs[1], 1, second)
+        project(acc0b, 0, second)
         grouped23 = late.tile([P, 2 * P, PACK], BF16, name="grouped23", offset=5120, align_bytes=64)
         nc.vector.tensor_copy(*interleaved(grouped23[:], raw23[:]))
-        nc.vector.tensor_copy(v0b[:, P:], acc0b[:, second])
-        v1 = keep.tile([P, I], F32, name="v1")
+        v1 = late.tile([P, I], F32, name="v1", offset=20480)
         nc.vector.tensor_copy(v1[:], accs[1][:])
         quantise(grouped23, w_codes[1][:], slice(2 * P, 4 * P))
-        nc.vector.tensor_copy(places(1, every), v1[:])
+        nc.vector.tensor_copy(v0b[:], acc0b[:, second])
+        nc.vector.tensor_copy(places(1, first), v1[:, first])
         accs.extend([bank("acc2", 6), bank("acc3", 7)])
         project(accs[2], 2, every)
         project(accs[3], 3, every)
-        v3a = keep.tile([P, split], F32, name="v3a", tag="after_lead")
-        nc.vector.tensor_copy(v3a[:], accs[3][:, lead])
+        v2a = keep.tile([P, HALF], F32, name="v2a")
+        nc.vector.tensor_copy(v2a[:], accs[2][:, first])
+        nc.vector.tensor_copy(places(1, second), v1[:, second])
         kept1 = early.tile([P, T], F32, name="kept1", offset=0)
-        for h in range(2):
-            keep_old(1, kept1[:, halves[h]], h)
+        keep_old(1, kept1[:, halves[0]], 0)
+        v3a = late.tile([P, split], F32, name="v3a", offset=20480)
+        nc.vector.tensor_copy(v3a[:], accs[3][:, lead])
+        keep_old(1, kept1[:, halves[1]], 1)
         nc.vector.tensor_copy(places(3, lead), v3a[:])
-        v2a = keep.tile([P, HALF], F32, name="v2a", tag="after_first_scatter")
-        nc.scalar.activation(places(0, slice(P, I)), v0b[:], COPY)
-        nc.scalar.copy(v2a[:], accs[2][:, first])
+        nc.scalar.activation(places(0, second), v0b[:], COPY)
         nc.scalar.activation(places(2, first), v2a[:], COPY)
         turned = bank("turned", 4, 2)
-        scaled = keep.tile([P, T], F32, name="scaled")
+        scaled = keep.tile([P, T], F32, name="scaled", tag="after_turn_back")
         blocks = [slice(m * P, (m + 1) * P) for m in range(T_BLOCKS)]
         for block in blocks:
             nc.tensor.transpose(turned[:, block], olds[2][:, block], identity[:])
@@ -212,20 +210,14 @@ def tile_attend_cachewrite_kernel(tc, emb_words, emb_scales, wv, old, retain, of
             nc.sync.dma_start(out=out[P : 2 * P, cols], in_=results[1][:, cols])
 
         nc.scalar.activation(places(3, rest), v3b[:], COPY)
-        kept3a = keep.tile([P, BANK], F32, name="kept3a", tag="old1")
-        keep_old(3, kept3a[:], 0)
-        kept3b = keep.tile([P, BANK], F32, name="kept3b", tag="after_lead")
-        keep_old(3, kept3b[:], 1)
-        result2 = keep.tile([P, T], F32, name="result2", tag="after_product3")
+        kept3 = late.tile([P, T], F32, name="kept3", offset=20480 + 1536)
+        keep_old(3, kept3[:, halves[0]], 0)
+        nc.gpsimd.tensor_tensor(kept3[:, halves[1]], olds[3][:, halves[1]], retain_wide[:, halves[1]], MULT)
+        result2 = keep.tile([P, T], F32, name="result2")
         for cols in halves:
             nc.vector.tensor_tensor(result2[:, cols], windows[2][:, cols], back[:, cols], ADD)
             nc.sync.dma_start(out=out[2 * P : 3 * P, cols], in_=result2[:, cols])
-        result3 = keep.tile([P, T], F32, name="result3", tag="window2")
-        pieces = (
-            (halves[0], kept3a[:]),
-            (slice(BANK, BANK + HALF), kept3b[:, 0:HALF]),
-            (slice(BANK + HALF, T), kept3b[:, HALF:BANK]),
-        )
-        for cols, kept3 in pieces:
-            nc.vector.tensor_tensor(result3[:, cols], kept3, windows[3][:, cols], ADD)
+        result3 = keep.tile([P, T], F32, name="result3", tag="after_turn_back")
+        for cols in (halves[0], slice(BANK, BANK + HALF), slice(BANK + HALF, T)):
+            nc.vector.tensor_tensor(result3[:, cols], kept3[:, cols], windows[3][:, cols], ADD)
             nc.scalar.dma_start(out=out[3 * P : 4 * P, cols], in_=result3[:, cols])

@@ -23,6 +23,7 @@ BANK = 512
 HALF = I // 2
 E_TILES = E // P
 T_BLOCKS = T // P
+SPLIT = 288
 
 
 def interleaved(dst, src):
@@ -48,10 +49,9 @@ def tile_attend_cachewrite_kernel(tc, emb_words, emb_scales, wv, old, retain, of
         w_planes = keep.tile([P, E], U8, name="w_planes", align_bytes=64)
         identity = keep.tile([P, P], F32, name="identity")
         retain_rows = early.tile([P, P], F32, name="retain_rows", offset=2080)
-        scale_cols = [
-            late.tile([P, 16], F32, name="scale_cols0", offset=16384),
-            keep.tile([P, 2], F32, name="scale_cols1"),
-        ]
+        v2 = keep.tile([P, I], F32, name="v2")
+        v3b = keep.tile([P, I - SPLIT], F32, name="v3b")
+        scale_cols = (v2[:, I - 4 :], v3b[:, 0:2])
         raw01 = keep.tile([P, PACK, 2 * P], F32, name="raw01", tag="after_interleave")
         raw23 = keep.tile([P, PACK, 2 * P], F32, name="raw23")
         windows = [keep.tile([P, T], F32, name=f"window{j}", tag=f"window{j}") for j in range(E_TILES)]
@@ -117,8 +117,8 @@ def tile_attend_cachewrite_kernel(tc, emb_words, emb_scales, wv, old, retain, of
         nc.tensor.transpose(turned_rows[:, 0:P], retain_rows[:], identity[:])
         spread_cols = keep.tile([P, T_BLOCKS], F32, name="spread_cols")
         nc.scalar.copy(spread_cols[:], turned_rows[:, 0:T_BLOCKS])
-        nc.scalar.copy(scale_cols[0][:, 0:6], turned_rows[:, 0:6])
-        nc.scalar.copy(scale_cols[1][:], turned_rows[:, 6:8])
+        nc.scalar.copy(scale_cols[0], turned_rows[:, 0:4])
+        nc.scalar.copy(scale_cols[1], turned_rows[:, 4:6])
         spread = [bank(f"spread{h}", h) for h in range(2)]
         for m in range(T_BLOCKS):
             nc.tensor.transpose(
@@ -150,7 +150,7 @@ def tile_attend_cachewrite_kernel(tc, emb_words, emb_scales, wv, old, retain, of
         def keep_old(j, kept, h):
             nc.vector.tensor_tensor(kept, olds[j][:, halves[h]], spread[h][:], MULT)
 
-        split = 288
+        split = SPLIT
         lead, rest = slice(0, split), slice(split, I)
         v0a = keep.tile([P, HALF], F32, name="v0a")
         v0b = keep.tile([P, HALF], F32, name="v0b")
@@ -169,13 +169,13 @@ def tile_attend_cachewrite_kernel(tc, emb_words, emb_scales, wv, old, retain, of
         nc.vector.tensor_copy(v1[:], accs[1][:])
         quantise(grouped23, w_codes[1][:], slice(2 * P, 4 * P))
         nc.vector.tensor_copy(v0b[:], acc0b[:, second])
-        nc.vector.tensor_copy(places(1, first), v1[:, first])
+        nc.vector.tensor_copy(places(1, slice(0, P)), v1[:, 0:P])
         accs.extend([bank("acc2", 6), bank("acc3", 7)])
         project(accs[2], 2, every)
         project(accs[3], 3, every)
-        v2a = keep.tile([P, HALF], F32, name="v2a")
-        nc.vector.tensor_copy(v2a[:], accs[2][:, first])
-        nc.vector.tensor_copy(places(1, second), v1[:, second])
+        most, tail = slice(0, I - 32), slice(I - 32, I)
+        nc.vector.tensor_copy(v2[:, most], accs[2][:, most])
+        nc.vector.tensor_copy(places(1, slice(P, I)), v1[:, P:])
         kept1 = early.tile([P, T], F32, name="kept1", offset=0)
         keep_old(1, kept1[:, halves[0]], 0)
         v3a = late.tile([P, split], F32, name="v3a", offset=20480)
@@ -183,22 +183,23 @@ def tile_attend_cachewrite_kernel(tc, emb_words, emb_scales, wv, old, retain, of
         keep_old(1, kept1[:, halves[1]], 1)
         nc.vector.tensor_copy(places(3, lead), v3a[:])
         nc.scalar.activation(places(0, second), v0b[:], COPY)
-        nc.scalar.activation(places(2, first), v2a[:], COPY)
+        nc.scalar.activation(places(2, first), v2[:, first], COPY)
         turned = bank("turned", 4, 2)
         scaled = keep.tile([P, T], F32, name="scaled", tag="after_turn_back")
         blocks = [slice(m * P, (m + 1) * P) for m in range(T_BLOCKS)]
         for block in blocks:
             nc.tensor.transpose(turned[:, block], olds[2][:, block], identity[:])
+        factors = [scale_cols[0][:, m : m + 1] for m in range(4)] + [scale_cols[1][:, m : m + 1] for m in range(2)]
+        factors.extend(spread_cols[:, m : m + 1] for m in (6, 7))
         for m, block in enumerate(blocks):
-            nc.scalar.activation(scaled[:, block], turned[:, block], COPY, scale=scale_cols[m // 6][:, m % 6 : m % 6 + 1])
-        v2b = late.tile([P, HALF], F32, name="v2b", offset=16384 + 32 - 1024)
-        v3b = late.tile([P, I - split], F32, name="v3b", offset=16384 + 32)
-        nc.scalar.copy(v2b[:], accs[2][:, second])
+            nc.scalar.activation(scaled[:, block], turned[:, block], COPY, scale=factors[m])
+            if m == 5:
+                nc.scalar.copy(v2[:, tail], accs[2][:, tail])
         nc.scalar.copy(v3b[:], accs[3][:, rest])
         back = bank("back", 2, 2)
         for block in blocks:
             nc.tensor.transpose(back[:, block], scaled[:, block], identity[:])
-        nc.scalar.activation(places(2, second), v2b[:], COPY)
+        nc.scalar.activation(places(2, second), v2[:, second], COPY)
 
         results = [keep.tile([P, T], F32, name=f"result{j}") for j in range(2)]
         kept0 = late.tile([P, T], F32, name="kept0", offset=2048)
@@ -211,8 +212,10 @@ def tile_attend_cachewrite_kernel(tc, emb_words, emb_scales, wv, old, retain, of
 
         nc.scalar.activation(places(3, rest), v3b[:], COPY)
         kept3 = late.tile([P, T], F32, name="kept3", offset=20480 + 1536)
+        share = BANK + P
         keep_old(3, kept3[:, halves[0]], 0)
-        nc.gpsimd.tensor_tensor(kept3[:, halves[1]], olds[3][:, halves[1]], retain_wide[:, halves[1]], MULT)
+        nc.vector.tensor_tensor(kept3[:, BANK:share], olds[3][:, BANK:share], spread[1][:, 0 : share - BANK], MULT)
+        nc.gpsimd.tensor_tensor(kept3[:, share:], olds[3][:, share:], retain_wide[:, share:], MULT)
         result2 = keep.tile([P, T], F32, name="result2")
         for cols in halves:
             nc.vector.tensor_tensor(result2[:, cols], windows[2][:, cols], back[:, cols], ADD)

@@ -23,7 +23,7 @@ BANK = 512
 HALF = I // 2
 E_TILES = E // P
 T_BLOCKS = T // P
-SPLIT = 288
+SPLIT = 352
 
 
 def interleaved(dst, src):
@@ -50,8 +50,9 @@ def tile_attend_cachewrite_kernel(tc, emb_words, emb_scales, wv, old, retain, of
         identity = keep.tile([P, P], F32, name="identity")
         retain_rows = early.tile([P, P], F32, name="retain_rows", offset=2080)
         v2 = keep.tile([P, I], F32, name="v2")
-        v3b = keep.tile([P, I - SPLIT], F32, name="v3b")
-        scale_cols = (v2[:, I - 4 :], v3b[:, 0:2])
+        v3a = keep.tile([P, HALF], F32, name="v3a")
+        v3b = keep.tile([P, HALF], F32, name="v3b", tag="after_last_scatter")
+        scale_cols = v3a[:, HALF - 4 :]
         raw01 = keep.tile([P, PACK, 2 * P], F32, name="raw01", tag="after_interleave")
         raw23 = keep.tile([P, PACK, 2 * P], F32, name="raw23")
         windows = [keep.tile([P, T], F32, name=f"window{j}", tag=f"window{j}") for j in range(E_TILES)]
@@ -117,8 +118,7 @@ def tile_attend_cachewrite_kernel(tc, emb_words, emb_scales, wv, old, retain, of
         nc.tensor.transpose(turned_rows[:, 0:P], retain_rows[:], identity[:])
         spread_cols = keep.tile([P, T_BLOCKS], F32, name="spread_cols")
         nc.scalar.copy(spread_cols[:], turned_rows[:, 0:T_BLOCKS])
-        nc.scalar.copy(scale_cols[0], turned_rows[:, 0:4])
-        nc.scalar.copy(scale_cols[1], turned_rows[:, 4:6])
+        nc.scalar.copy(scale_cols, turned_rows[:, 0:4])
         spread = [bank(f"spread{h}", h) for h in range(2)]
         for m in range(T_BLOCKS):
             nc.tensor.transpose(
@@ -161,47 +161,60 @@ def tile_attend_cachewrite_kernel(tc, emb_words, emb_scales, wv, old, retain, of
         project(accs[1], 1, first)
         nc.scalar.copy(v0a[:], accs[0][:, first])
         nc.scalar.activation(places(0, first), v0a[:], COPY)
-        project(accs[1], 1, second)
+        acc1b = bank("acc1b", 3)
         project(acc0b, 0, second)
+        project(acc1b, 1, second)
         grouped23 = late.tile([P, 2 * P, PACK], BF16, name="grouped23", offset=5120, align_bytes=64)
         nc.vector.tensor_copy(*interleaved(grouped23[:], raw23[:]))
-        v1 = late.tile([P, I], F32, name="v1", offset=20480)
-        nc.vector.tensor_copy(v1[:], accs[1][:])
+        v1a = late.tile([P, HALF], F32, name="v1a", offset=20480)
+        v1b = late.tile([P, HALF], F32, name="v1b", offset=6144)
+        nc.vector.tensor_copy(v1a[:], accs[1][:, first])
         quantise(grouped23, w_codes[1][:], slice(2 * P, 4 * P))
+        nc.scalar.copy(v1b[:], acc1b[:, second])
         nc.vector.tensor_copy(v0b[:], acc0b[:, second])
-        nc.vector.tensor_copy(places(1, slice(0, P)), v1[:, 0:P])
+        nc.vector.tensor_copy(places(1, first), v1a[:])
         accs.extend([bank("acc2", 6), bank("acc3", 7)])
         project(accs[2], 2, every)
         project(accs[3], 3, every)
-        most, tail = slice(0, I - 32), slice(I - 32, I)
-        nc.vector.tensor_copy(v2[:, most], accs[2][:, most])
-        nc.vector.tensor_copy(places(1, slice(P, I)), v1[:, P:])
+        nc.vector.tensor_copy(v2[:], accs[2][:])
+        most, tail = slice(0, HALF - 32), slice(HALF - 32, HALF)
+        nc.vector.tensor_copy(v3a[:, most], accs[3][:, most])
+        nc.vector.tensor_copy(places(1, second), v1b[:])
         kept1 = early.tile([P, T], F32, name="kept1", offset=0)
         keep_old(1, kept1[:, halves[0]], 0)
-        v3a = late.tile([P, split], F32, name="v3a", offset=20480)
-        nc.vector.tensor_copy(v3a[:], accs[3][:, lead])
         keep_old(1, kept1[:, halves[1]], 1)
-        nc.vector.tensor_copy(places(3, lead), v3a[:])
         nc.scalar.activation(places(0, second), v0b[:], COPY)
-        nc.scalar.activation(places(2, first), v2[:, first], COPY)
-        turned = bank("turned", 4, 2)
-        scaled = keep.tile([P, T], F32, name="scaled", tag="after_turn_back")
-        blocks = [slice(m * P, (m + 1) * P) for m in range(T_BLOCKS)]
-        for block in blocks:
-            nc.tensor.transpose(turned[:, block], olds[2][:, block], identity[:])
-        factors = [scale_cols[0][:, m : m + 1] for m in range(4)] + [scale_cols[1][:, m : m + 1] for m in range(2)]
-        factors.extend(spread_cols[:, m : m + 1] for m in (6, 7))
-        for m, block in enumerate(blocks):
-            nc.scalar.activation(scaled[:, block], turned[:, block], COPY, scale=factors[m])
-            if m == 5:
-                nc.scalar.copy(v2[:, tail], accs[2][:, tail])
-        nc.scalar.copy(v3b[:], accs[3][:, rest])
-        back = bank("back", 2, 2)
-        for block in blocks:
-            nc.tensor.transpose(back[:, block], scaled[:, block], identity[:])
-        nc.scalar.activation(places(2, second), v2[:, second], COPY)
+        nc.scalar.activation(places(2, rest), v2[:, rest], COPY)
+        nc.vector.tensor_copy(places(2, lead), v2[:, lead])
 
-        results = [keep.tile([P, T], F32, name=f"result{j}") for j in range(2)]
+        blocks = [slice(m * P, (m + 1) * P) for m in range(T_BLOCKS)]
+        scaled = [keep.tile([P, BANK], F32, name=f"scaled{h}", tag=f"after_turn_back{h}") for h in range(2)]
+
+        def turn(dst, ms):
+            for n, m in enumerate(ms):
+                nc.tensor.transpose(dst[:, blocks[n]], olds[2][:, blocks[m]], identity[:])
+
+        def scale(src, ms, factors):
+            for n, m in enumerate(ms):
+                nc.scalar.activation(scaled[m // 4][:, blocks[m % 4]], src[:, blocks[n]], COPY, scale=factors[:, n : n + 1])
+
+        turned = [bank("turned0", 4), bank("turned1", 5)]
+        turn(turned[0], (0, 1, 2, 3))
+        turn(turned[1], (4, 5, 6, 7))
+        scale(turned[0], (0, 1, 2, 3), scale_cols)
+        nc.scalar.copy(v3a[:, tail], accs[3][:, tail])
+        nc.scalar.copy(v3b[:], accs[3][:, second])
+        scale(turned[1], (4, 5), spread_cols[:, 4:6])
+        back = [bank("back0", 2), bank("back1", 3)]
+        for m in range(4):
+            nc.tensor.transpose(back[0][:, blocks[m]], scaled[0][:, blocks[m]], identity[:])
+        nc.scalar.activation(places(3, first), v3a[:], COPY)
+        scale(turned[1][:, HALF:], (6, 7), spread_cols[:, 6:8])
+        for m in range(4):
+            nc.tensor.transpose(back[1][:, blocks[m]], scaled[1][:, blocks[m]], identity[:])
+        nc.scalar.activation(places(3, second), v3b[:], COPY)
+
+        results = [keep.tile([P, T], F32, name=f"result{j}") for j in range(E_TILES)]
         kept0 = late.tile([P, T], F32, name="kept0", offset=2048)
         nc.gpsimd.tensor_tensor(kept0[:], olds[0][:], retain_wide[:], MULT)
         nc.gpsimd.tensor_tensor(results[0][:], kept0[:], windows[0][:], ADD)
@@ -210,17 +223,25 @@ def tile_attend_cachewrite_kernel(tc, emb_words, emb_scales, wv, old, retain, of
             nc.gpsimd.tensor_tensor(results[1][:, cols], kept1[:, cols], windows[1][:, cols], ADD)
             nc.sync.dma_start(out=out[P : 2 * P, cols], in_=results[1][:, cols])
 
-        nc.scalar.activation(places(3, rest), v3b[:], COPY)
-        kept3 = late.tile([P, T], F32, name="kept3", offset=20480 + 1536)
-        share = BANK + P
-        keep_old(3, kept3[:, halves[0]], 0)
-        nc.vector.tensor_tensor(kept3[:, BANK:share], olds[3][:, BANK:share], spread[1][:, 0 : share - BANK], MULT)
-        nc.gpsimd.tensor_tensor(kept3[:, share:], olds[3][:, share:], retain_wide[:, share:], MULT)
-        result2 = keep.tile([P, T], F32, name="result2")
-        for cols in halves:
-            nc.vector.tensor_tensor(result2[:, cols], windows[2][:, cols], back[:, cols], ADD)
-            nc.sync.dma_start(out=out[2 * P : 3 * P, cols], in_=result2[:, cols])
-        result3 = keep.tile([P, T], F32, name="result3", tag="after_turn_back")
-        for cols in (halves[0], slice(BANK, BANK + HALF), slice(BANK + HALF, T)):
-            nc.vector.tensor_tensor(result3[:, cols], kept3[:, cols], windows[3][:, cols], ADD)
-            nc.scalar.dma_start(out=out[3 * P : 4 * P, cols], in_=result3[:, cols])
+        own, shared, last = slice(0, 3 * P), slice(3 * P, 6 * P), slice(6 * P, T)
+        kept3a = keep.tile([P, 3 * P], F32, name="kept3a", tag="after_turn_back0")
+        kept3b = late.tile([P, 3 * P], F32, name="kept3b", offset=6144)
+        turned3, back3 = bank("turned3", 4), bank("back3", 6)
+        for n in range(2):
+            nc.tensor.transpose(turned3[:, blocks[n]], olds[3][:, blocks[6 + n]], identity[:])
+        scaled3 = keep.tile([P, HALF], F32, name="scaled3", tag="after_last_scatter")
+        for n in range(2):
+            nc.scalar.activation(scaled3[:, blocks[n]], turned3[:, blocks[n]], COPY, scale=spread_cols[:, 6 + n : 7 + n])
+            nc.tensor.transpose(back3[:, blocks[n]], scaled3[:, blocks[n]], identity[:])
+
+        def add_back(h):
+            nc.vector.tensor_tensor(results[2][:, halves[h]], windows[2][:, halves[h]], back[h][:], ADD)
+            nc.sync.dma_start(out=out[2 * P : 3 * P, halves[h]], in_=results[2][:, halves[h]])
+
+        add_back(0)
+        nc.vector.tensor_tensor(kept3a[:], olds[3][:, own], spread[0][:, own], MULT)
+        add_back(1)
+        nc.gpsimd.tensor_tensor(kept3b[:], olds[3][:, shared], retain_wide[:, shared], MULT)
+        for kept, cols in ((kept3a[:], own), (kept3b[:], shared), (back3[:, 0:HALF], last)):
+            nc.vector.tensor_tensor(results[3][:, cols], windows[3][:, cols], kept, ADD)
+            nc.sync.dma_start(out=out[3 * P : 4 * P, cols], in_=results[3][:, cols])

@@ -48,14 +48,14 @@ def tile_attend_cachewrite_kernel(tc, emb_words, emb_scales, wv, old, retain, of
         planes = keep.tile([P, U], U8, name="planes", tag="after_scale_gather", align_bytes=64)
         w_planes = keep.tile([P, E], U8, name="w_planes", align_bytes=64)
         identity = keep.tile([P, P], F32, name="identity")
-        retain_rows = early.tile([P, P], F32, name="retain_rows", offset=2080)
+        retain_rows = early.tile([P, P], F32, name="retain_rows", offset=6144)
         v2 = keep.tile([P, I], F32, name="v2")
         v3a = keep.tile([P, HALF], F32, name="v3a")
         v3b = keep.tile([P, HALF], F32, name="v3b", tag="after_last_scatter")
         scale_cols = v3a[:, HALF - 4 :]
         raw01 = keep.tile([P, PACK, 2 * P], F32, name="raw01", tag="after_interleave")
         raw23 = keep.tile([P, PACK, 2 * P], F32, name="raw23")
-        windows = [keep.tile([P, T], F32, name=f"window{j}", tag=f"window{j}") for j in range(E_TILES)]
+        windows = [keep.tile([P, T], F32, name=f"window{j}", tag=f"window{j}") for j in range(3)]
         olds = [
             keep.tile([P, T], F32, name="old0"),
             keep.tile([P, T], F32, name="old1"),
@@ -127,8 +127,8 @@ def tile_attend_cachewrite_kernel(tc, emb_words, emb_scales, wv, old, retain, of
                 identity[:],
             )
 
-        grouped0 = early.tile([P, P, PACK], BF16, name="grouped0", offset=0, align_bytes=64)
-        grouped1 = early.tile([P, P, PACK], BF16, name="grouped1", offset=1088, align_bytes=64)
+        grouped0 = early.tile([P, P, PACK], BF16, name="grouped0", offset=4096, align_bytes=64)
+        grouped1 = early.tile([P, P, PACK], BF16, name="grouped1", offset=5632, align_bytes=64)
         nc.scalar.copy(*interleaved(grouped1[:], raw01[:, :, P : 2 * P]))
         nc.vector.tensor_copy(*interleaved(grouped0[:], raw01[:, :, 0:P]))
         retain_wide = keep.tile([P, T], F32, name="retain_wide", tag="after_interleave")
@@ -142,8 +142,10 @@ def tile_attend_cachewrite_kernel(tc, emb_words, emb_scales, wv, old, retain, of
         ]
         quantise(grouped0, w_codes[0][:, 0:P], slice(0, P))
         quantise(grouped1, w_codes[0][:, P : 2 * P], slice(P, 2 * P))
+        windows.append(early.tile([P, T], F32, name="window3", offset=6144))
+        nc.gpsimd.memset(windows[3][:].bitcast(I32), 0)
 
-        picked_words = early.tile([P, I], U32, name="picked_words", offset=0, align_bytes=64)
+        picked_words = early.tile([P, I], U32, name="picked_words", offset=4096, align_bytes=64)
         nc.vector.tensor_copy(picked_words[:, first], words[:].indirect(gather_list[:, 0 : HALF // 16]))
         nc.vector.tensor_copy(picked_words[:, second], words[:].indirect(gather_list[:, HALF // 16 : I // 16]))
 
@@ -180,7 +182,7 @@ def tile_attend_cachewrite_kernel(tc, emb_words, emb_scales, wv, old, retain, of
         most, tail = slice(0, HALF - 32), slice(HALF - 32, HALF)
         nc.vector.tensor_copy(v3a[:, most], accs[3][:, most])
         nc.vector.tensor_copy(places(1, second), v1b[:])
-        kept1 = early.tile([P, T], F32, name="kept1", offset=0)
+        kept1 = early.tile([P, T], F32, name="kept1", offset=1024)
         keep_old(1, kept1[:, halves[0]], 0)
         keep_old(1, kept1[:, halves[1]], 1)
         nc.scalar.activation(places(0, second), v0b[:], COPY)

@@ -23,7 +23,7 @@ BANK = 512
 HALF = I // 2
 E_TILES = E // P
 T_BLOCKS = T // P
-SPLIT = 352
+SPLIT = 320
 
 
 def interleaved(dst, src):
@@ -50,8 +50,8 @@ def tile_attend_cachewrite_kernel(tc, emb_words, emb_scales, wv, old, retain, of
         identity = keep.tile([P, P], F32, name="identity")
         retain_rows = early.tile([P, P], F32, name="retain_rows", offset=6144)
         v2 = keep.tile([P, I], F32, name="v2")
-        v3a = keep.tile([P, HALF], F32, name="v3a")
-        v3b = keep.tile([P, HALF], F32, name="v3b", tag="after_last_scatter")
+        v3a = keep.tile([P, HALF], F32, name="v3a", tag="after_last_scatter")
+        v3b = keep.tile([P, HALF], F32, name="v3b")
         scale_cols = v3a[:, HALF - 4 :]
         raw01 = keep.tile([P, PACK, 2 * P], F32, name="raw01", tag="after_interleave")
         raw23 = keep.tile([P, PACK, 2 * P], F32, name="raw23")

@@ -23,6 +23,7 @@ BANK = 512
 HALF = I // 2
 E_TILES = E // P
 T_BLOCKS = T // P
+TOP = P - T_BLOCKS
 SPLIT = 320
 
 
@@ -63,18 +64,18 @@ def tile_attend_cachewrite_kernel(tc, emb_words, emb_scales, wv, old, retain, of
             keep.tile([P, T], F32, name="old3"),
         ]
 
-        nc.vector.memset(retain_rows[:], 0.0)
         nc.vector.memset(planes[:].bitcast(I32), 0)
+        nc.vector.memset(retain_rows[0:TOP, :], 0.0)
         make_identity(nc, identity[:])
         for window in windows:
             nc.vector.memset(window[:].bitcast(I32), 0)
 
         wv_rows = wv.rearrange("(p r) e -> p r e", r=PACK)
         nc.sync.dma_start(out=raw01[:], in_=wv_rows[:, :, 0 : 2 * P])
-        nc.sync.dma_start(out=retain_rows[0:T_BLOCKS, :], in_=retain.rearrange("o (m n) -> (o m) n", n=P))
+        nc.scalar.dma_start(out=retain_rows[TOP:P, :], in_=retain.rearrange("o (m n) -> (o m) n", n=P))
         nc.sync.dma_start(gather_list[:], offs)
         for r in range(4):
-            nc.sync.dma_start(
+            (nc.sync if r < 3 else nc.scalar).dma_start(
                 out=planes[r:P:32, :].bitcast(I32),
                 in_=emb_scales[0, r:16:4, :].bitcast(I32),
             )
@@ -117,8 +118,8 @@ def tile_attend_cachewrite_kernel(tc, emb_words, emb_scales, wv, old, retain, of
         turned_rows = bank("turned_rows", 2)
         nc.tensor.transpose(turned_rows[:, 0:P], retain_rows[:], identity[:])
         spread_cols = keep.tile([P, T_BLOCKS], F32, name="spread_cols")
-        nc.scalar.copy(spread_cols[:], turned_rows[:, 0:T_BLOCKS])
-        nc.scalar.copy(scale_cols, turned_rows[:, 0:4])
+        nc.scalar.copy(spread_cols[:], turned_rows[:, TOP:P])
+        nc.scalar.copy(scale_cols, turned_rows[:, TOP : TOP + 4])
         spread = [bank(f"spread{h}", h) for h in range(2)]
         for m in range(T_BLOCKS):
             nc.tensor.transpose(

@@ -222,7 +222,7 @@ def tile_attend_cachewrite_kernel(tc, emb_words, emb_scales, wv, old, retain, of
         nc.gpsimd.tensor_tensor(kept0[:], olds[0][:], retain_wide[:], MULT)
         nc.gpsimd.tensor_tensor(results[0][:], kept0[:], windows[0][:], ADD)
         nc.sync.dma_start(out=out[0:P, :], in_=results[0][:])
-        for cols in halves:
+        for cols in (halves[0], slice(4 * P, 6 * P), slice(6 * P, T)):
             nc.gpsimd.tensor_tensor(results[1][:, cols], kept1[:, cols], windows[1][:, cols], ADD)
             nc.sync.dma_start(out=out[P : 2 * P, cols], in_=results[1][:, cols])
 

@@ -25,6 +25,7 @@ E_TILES = E // P
 T_BLOCKS = T // P
 TOP = P - T_BLOCKS
 SPLIT = 320
+ROW = 256
 
 
 def interleaved(dst, src):
@@ -45,8 +46,8 @@ def tile_attend_cachewrite_kernel(tc, emb_words, emb_scales, wv, old, retain, of
 
         gather_list = keep.tile([P, I // 16], U16, name="gather_list")
         scatter_list = keep.tile([P, I // 16], U16, name="scatter_list")
-        words = late.tile([P, U], U32, name="words", offset=2048, align_bytes=64)
-        planes = keep.tile([P, U], U8, name="planes", tag="after_scale_gather", align_bytes=64)
+        words = late.tile([P, U], U32, name="words", offset=2048, align_bytes=ROW)
+        planes = keep.tile([P, U], U8, name="planes", tag="after_scale_gather", align_bytes=ROW)
         w_planes = keep.tile([P, E], U8, name="w_planes", align_bytes=64)
         identity = keep.tile([P, P], F32, name="identity")
         retain_rows = early.tile([P, P], F32, name="retain_rows", offset=6144)
@@ -54,14 +55,14 @@ def tile_attend_cachewrite_kernel(tc, emb_words, emb_scales, wv, old, retain, of
         v3a = keep.tile([P, HALF], F32, name="v3a", tag="after_last_scatter")
         v3b = keep.tile([P, HALF], F32, name="v3b")
         scale_cols = v3a[:, HALF - 4 :]
-        raw01 = keep.tile([P, PACK, 2 * P], F32, name="raw01", tag="after_interleave")
-        raw23 = keep.tile([P, PACK, 2 * P], F32, name="raw23")
+        raw01 = keep.tile([P, PACK, 2 * P], F32, name="raw01", tag="after_interleave", align_bytes=ROW)
+        raw23 = keep.tile([P, PACK, 2 * P], F32, name="raw23", align_bytes=ROW)
         windows = [keep.tile([P, T], F32, name=f"window{j}", tag=f"window{j}") for j in range(3)]
         olds = [
-            keep.tile([P, T], F32, name="old0"),
-            keep.tile([P, T], F32, name="old1"),
-            keep.tile([P, T], F32, name="old2"),
-            keep.tile([P, T], F32, name="old3"),
+            keep.tile([P, T], F32, name="old0", align_bytes=ROW),
+            keep.tile([P, T], F32, name="old1", align_bytes=ROW),
+            keep.tile([P, T], F32, name="old2", align_bytes=ROW),
+            keep.tile([P, T], F32, name="old3", align_bytes=ROW),
         ]
 
         nc.vector.memset(planes[:].bitcast(I32), 0)
@@ -132,13 +133,13 @@ def tile_attend_cachewrite_kernel(tc, emb_words, emb_scales, wv, old, retain, of
         grouped1 = early.tile([P, P, PACK], BF16, name="grouped1", offset=5632, align_bytes=64)
         nc.scalar.copy(*interleaved(grouped1[:], raw01[:, :, P : 2 * P]))
         nc.vector.tensor_copy(*interleaved(grouped0[:], raw01[:, :, 0:P]))
-        retain_wide = keep.tile([P, T], F32, name="retain_wide", tag="after_interleave")
+        retain_wide = keep.tile([P, T], F32, name="retain_wide", tag="after_interleave", align_bytes=ROW)
         for h in range(2):
             nc.scalar.copy(retain_wide[:, halves[h]], spread[h][:])
         picked_planes = keep.tile([P, I], U8, name="picked_planes", align_bytes=64)
         nc.vector.tensor_copy(picked_planes[:], planes[:].indirect(gather_list[:]))
         w_codes = [
-            keep.tile([P, 2 * P], U32, name="codes01", tag="after_scale_gather", align_bytes=64),
+            keep.tile([P, 2 * P], U32, name="codes01", tag="after_scale_gather", align_bytes=ROW),
             keep.tile([P, 2 * P], U32, name="codes23", align_bytes=64),
         ]
         quantise(grouped0, w_codes[0][:, 0:P], slice(0, P))
@@ -217,7 +218,7 @@ def tile_attend_cachewrite_kernel(tc, emb_words, emb_scales, wv, old, retain, of
             nc.tensor.transpose(back[1][:, blocks[m]], scaled[1][:, blocks[m]], identity[:])
         nc.scalar.activation(places(3, second), v3b[:], COPY)
 
-        results = [keep.tile([P, T], F32, name=f"result{j}") for j in range(E_TILES)]
+        results = [keep.tile([P, T], F32, name=f"result{j}", align_bytes=ROW) for j in range(E_TILES)]
         kept0 = late.tile([P, T], F32, name="kept0", offset=2048)
         nc.gpsimd.tensor_tensor(kept0[:], olds[0][:], retain_wide[:], MULT)
         nc.gpsimd.tensor_tensor(results[0][:], kept0[:], windows[0][:], ADD)

@@ -52,7 +52,7 @@ def tile_attend_cachewrite_kernel(tc, emb_words, emb_scales, wv, old, retain, of
         identity = keep.tile([P, P], F32, name="identity")
         retain_rows = early.tile([P, P], F32, name="retain_rows", offset=6144)
         v2 = keep.tile([P, I], F32, name="v2")
-        v3a = keep.tile([P, HALF], F32, name="v3a", tag="after_last_scatter")
+        v3a = keep.tile([P, HALF], F32, name="v3a")
         v3b = keep.tile([P, HALF], F32, name="v3b")
         scale_cols = v3a[:, HALF - 4 :]
         raw01 = keep.tile([P, PACK, 2 * P], F32, name="raw01", tag="after_interleave", align_bytes=ROW)
@@ -230,13 +230,7 @@ def tile_attend_cachewrite_kernel(tc, emb_words, emb_scales, wv, old, retain, of
         own, shared, last = slice(0, 3 * P), slice(3 * P, 6 * P), slice(6 * P, T)
         kept3a = keep.tile([P, 3 * P], F32, name="kept3a", tag="after_turn_back0")
         kept3b = late.tile([P, 3 * P], F32, name="kept3b", offset=6144)
-        turned3, back3 = bank("turned3", 4), bank("back3", 6)
-        for n in range(2):
-            nc.tensor.transpose(turned3[:, blocks[n]], olds[3][:, blocks[6 + n]], identity[:])
-        scaled3 = keep.tile([P, HALF], F32, name="scaled3", tag="after_last_scatter")
-        for n in range(2):
-            nc.scalar.activation(scaled3[:, blocks[n]], turned3[:, blocks[n]], COPY, scale=spread_cols[:, 6 + n : 7 + n])
-            nc.tensor.transpose(back3[:, blocks[n]], scaled3[:, blocks[n]], identity[:])
+        kept3c = keep.tile([P, HALF], F32, name="kept3c", tag="after_turn_back1")
 
         def add_back(h):
             nc.vector.tensor_tensor(results[2][:, halves[h]], windows[2][:, halves[h]], back[h][:], ADD)
@@ -245,7 +239,8 @@ def tile_attend_cachewrite_kernel(tc, emb_words, emb_scales, wv, old, retain, of
         add_back(0)
         nc.vector.tensor_tensor(kept3a[:], olds[3][:, own], spread[0][:, own], MULT)
         add_back(1)
+        nc.vector.tensor_tensor(kept3c[:], olds[3][:, last], spread[1][:, HALF:], MULT)
         nc.gpsimd.tensor_tensor(kept3b[:], olds[3][:, shared], retain_wide[:, shared], MULT)
-        for kept, cols in ((kept3a[:], own), (kept3b[:], shared), (back3[:, 0:HALF], last)):
+        for kept, cols in ((kept3a[:], own), (kept3b[:], shared), (kept3c[:], last)):
             nc.vector.tensor_tensor(results[3][:, cols], windows[3][:, cols], kept, ADD)
             nc.sync.dma_start(out=out[3 * P : 4 * P, cols], in_=results[3][:, cols])

from contextlib import ExitStack

import concourse.mybir as mybir
from concourse.masks import make_identity

K, U, I, T, E = 512, 2048, 512, 1024, 512
FLOPS = 2 * K * E * I

F32 = mybir.dt.float32
BF16 = mybir.dt.bfloat16
I32 = mybir.dt.int32
U32 = mybir.dt.uint32
U16 = mybir.dt.uint16
U8 = mybir.dt.uint8
FP8X4 = mybir.dt.float8_e4m3fn_x4
COPY = mybir.ActivationFunctionType.Copy
MULT = mybir.AluOpType.mult
ADD = mybir.AluOpType.add

P = 128
PACK = 4
BANK = 512
HALF = I // 2
E_TILES = E // P
T_BLOCKS = T // P
TOP = P - T_BLOCKS
SPLIT = 320
ROW = 256


def interleaved(dst, src):
    return (
        dst.rearrange("p (c i) r -> p c r i", i=4),
        src.rearrange("p r (c i) -> p c r i", i=4),
    )


def tile_attend_cachewrite_kernel(tc, emb_words, emb_scales, wv, old, retain, offs, offs2, out):
    nc = tc.nc

    with ExitStack() as ctx:
        keep = ctx.enter_context(tc.tile_pool(name="keep", bufs=1))
        late = ctx.enter_context(tc.tile_pool(name="late", bufs=1))
        early = ctx.enter_context(tc.tile_pool(name="early", bufs=1))
        psum = ctx.enter_context(tc.psum_pool(name="psum", bufs=1))

        gather_list = keep.tile([P, I // 16], U16, name="gather_list")
        scatter_list = keep.tile([P, I // 16], U16, name="scatter_list")
        words = late.tile([P, U], U32, name="words", offset=2048, align_bytes=ROW)
        planes = keep.tile([P, U], U8, name="planes", tag="after_scale_gather", align_bytes=ROW)
        w_planes = keep.tile([P, E], U8, name="w_planes", align_bytes=64)
        identity = keep.tile([P, P], F32, name="identity")
        retain_rows = early.tile([P, P], F32, name="retain_rows", offset=6144)
        v2 = keep.tile([P, I], F32, name="v2")
        v3a = keep.tile([P, HALF], F32, name="v3a")
        v3b = keep.tile([P, HALF], F32, name="v3b")
        scale_cols = v3a[:, HALF - 4 :]
        raw01 = keep.tile([P, PACK, 2 * P], F32, name="raw01", tag="after_interleave", align_bytes=ROW)
        raw23 = keep.tile([P, PACK, 2 * P], F32, name="raw23", align_bytes=ROW)
        windows = [keep.tile([P, T], F32, name=f"window{j}", tag=f"window{j}") for j in range(3)]
        olds = [
            keep.tile([P, T], F32, name="old0", align_bytes=ROW),
            keep.tile([P, T], F32, name="old1", align_bytes=ROW),
            keep.tile([P, T], F32, name="old2", align_bytes=ROW),
            keep.tile([P, T], F32, name="old3", align_bytes=ROW),
        ]

        nc.vector.memset(planes[:].bitcast(I32), 0)
        nc.vector.memset(retain_rows[0:TOP, :], 0.0)
        make_identity(nc, identity[:])
        for window in windows:
            nc.vector.memset(window[:].bitcast(I32), 0)

        wv_rows = wv.rearrange("(p r) e -> p r e", r=PACK)
        nc.sync.dma_start(out=raw01[:], in_=wv_rows[:, :, 0 : 2 * P])
        nc.scalar.dma_start(out=retain_rows[TOP:P, :], in_=retain.rearrange("o (m n) -> (o m) n", n=P))
        nc.sync.dma_start(gather_list[:], offs)
        for r in range(4):
            (nc.sync if r < 3 else nc.scalar).dma_start(
                out=planes[r:P:32, :].bitcast(I32),
                in_=emb_scales[0, r:16:4, :].bitcast(I32),
            )
        nc.sync.dma_start(
            out=words[:].bitcast(I32),
            in_=emb_words[0].rearrange("p c r -> p (c r)").bitcast(I32),
        )
        nc.sync.dma_start(out=raw23[:], in_=wv_rows[:, :, 2 * P : 4 * P])
        nc.sync.dma_start(scatter_list[:], offs2)
        for j in range(E_TILES):
            nc.sync.dma_start(out=olds[j][:], in_=old[j * P : (j + 1) * P, :])

        def quantise(grouped, codes, cols):
            nc.vector.quantize_mx(
                out=codes.bitcast(FP8X4),
                scales=w_planes[:, cols],
                in_=grouped[:].rearrange("p c r -> p (c r)"),
            )

        def project(acc, j, slots):
            nc.tensor.matmul_mx(
                out=acc[:, slots],
                lhsT=w_codes[j // 2][:, (j % 2) * P : (j % 2 + 1) * P].bitcast(FP8X4),
                lhsT_scale=w_planes[:, j * P : (j + 1) * P],
                rhs=picked_words[:, slots].bitcast(FP8X4),
                rhs_scale=picked_planes[:, slots],
                start=True,
                stop=True,
            )

        def places(j, slots):
            return windows[j][:].indirect(scatter_list[:, slots.start // 16 : slots.stop // 16])

        first, second, every = slice(0, HALF), slice(HALF, I), slice(0, I)
        halves = (slice(0, BANK), slice(BANK, T))

        def bank(name, number, count=1):
            return psum.tile([P, count * BANK], F32, name=name, offset=number * BANK * 4)

        turned_rows = bank("turned_rows", 2)
        nc.tensor.transpose(turned_rows[:, 0:P], retain_rows[:], identity[:])
        spread_cols = keep.tile([P, T_BLOCKS], F32, name="spread_cols")
        nc.scalar.copy(spread_cols[:], turned_rows[:, TOP:P])
        nc.scalar.copy(scale_cols, turned_rows[:, TOP : TOP + 4])
        spread = [bank(f"spread{h}", h) for h in range(2)]
        for m in range(T_BLOCKS):
            nc.tensor.transpose(
                spread[m // 4][:, (m % 4) * P : (m % 4 + 1) * P],
                spread_cols[:, m : m + 1].to_broadcast([P, P]),
                identity[:],
            )

        grouped0 = early.tile([P, P, PACK], BF16, name="grouped0", offset=4096, align_bytes=64)
        grouped1 = early.tile([P, P, PACK], BF16, name="grouped1", offset=5632, align_bytes=64)
        nc.scalar.copy(*interleaved(grouped1[:], raw01[:, :, P : 2 * P]))
        nc.vector.tensor_copy(*interleaved(grouped0[:], raw01[:, :, 0:P]))
        retain_wide = keep.tile([P, T], F32, name="retain_wide", tag="after_interleave", align_bytes=ROW)
        for h in range(2):
            nc.scalar.copy(retain_wide[:, halves[h]], spread[h][:])
        picked_planes = keep.tile([P, I], U8, name="picked_planes", align_bytes=64)
        nc.vector.tensor_copy(picked_planes[:], planes[:].indirect(gather_list[:]))
        w_codes = [
            keep.tile([P, 2 * P], U32, name="codes01", tag="after_scale_gather", align_bytes=ROW),
            keep.tile([P, 2 * P], U32, name="codes23", align_bytes=64),
        ]
        quantise(grouped0, w_codes[0][:, 0:P], slice(0, P))
        quantise(grouped1, w_codes[0][:, P : 2 * P], slice(P, 2 * P))
        windows.append(early.tile([P, T], F32, name="window3", offset=6144))
        nc.gpsimd.memset(windows[3][:].bitcast(I32), 0)

        picked_words = early.tile([P, I], U32, name="picked_words", offset=4096, align_bytes=64)
        nc.vector.tensor_copy(picked_words[:, first], words[:].indirect(gather_list[:, 0 : HALF // 16]))
        nc.vector.tensor_copy(picked_words[:, second], words[:].indirect(gather_list[:, HALF // 16 : I // 16]))

        def keep_old(j, kept, h):
            nc.vector.tensor_tensor(kept, olds[j][:, halves[h]], spread[h][:], MULT)

        split = SPLIT
        lead, rest = slice(0, split), slice(split, I)
        v0a = keep.tile([P, HALF], F32, name="v0a")
        v0b = keep.tile([P, HALF], F32, name="v0b")
        accs = [bank(f"acc{j}", number) for j, number in enumerate((2, 4))]
        acc0b = bank("acc0b", 5)

        project(accs[0], 0, first)
        project(accs[1], 1, first)
        nc.scalar.copy(v0a[:], accs[0][:, first])
        nc.scalar.activation(places(0, first), v0a[:], COPY)
        acc1b = bank("acc1b", 3)
        project(acc0b, 0, second)
        project(acc1b, 1, second)
        grouped23 = late.tile([P, 2 * P, PACK], BF16, name="grouped23", offset=5120, align_bytes=64)
        nc.vector.tensor_copy(*interleaved(grouped23[:], raw23[:]))
        v1a = late.tile([P, HALF], F32, name="v1a", offset=20480)
        v1b = late.tile([P, HALF], F32, name="v1b", offset=6144)
        nc.vector.tensor_copy(v1a[:], accs[1][:, first])
        quantise(grouped23, w_codes[1][:], slice(2 * P, 4 * P))
        nc.scalar.copy(v1b[:], acc1b[:, second])
        nc.vector.tensor_copy(v0b[:], acc0b[:, second])
        nc.vector.tensor_copy(places(1, first), v1a[:])
        accs.extend([bank("acc2", 6), bank("acc3", 7)])
        project(accs[2], 2, every)
        project(accs[3], 3, every)
        nc.vector.tensor_copy(v2[:], accs[2][:])
        most, tail = slice(0, HALF - 32), slice(HALF - 32, HALF)
        nc.vector.tensor_copy(v3a[:, most], accs[3][:, most])
        nc.vector.tensor_copy(places(1, second), v1b[:])
        kept1 = early.tile([P, T], F32, name="kept1", offset=1024)
        keep_old(1, kept1[:, halves[0]], 0)
        keep_old(1, kept1[:, halves[1]], 1)
        nc.scalar.activation(places(0, second), v0b[:], COPY)
        nc.scalar.activation(places(2, rest), v2[:, rest], COPY)
        nc.vector.tensor_copy(places(2, lead), v2[:, lead])

        blocks = [slice(m * P, (m + 1) * P) for m in range(T_BLOCKS)]
        scaled = [keep.tile([P, BANK], F32, name=f"scaled{h}", tag=f"after_turn_back{h}") for h in range(2)]

        def turn(dst, ms):
            for n, m in enumerate(ms):
                nc.tensor.transpose(dst[:, blocks[n]], olds[2][:, blocks[m]], identity[:])

        def scale(src, ms, factors):
            for n, m in enumerate(ms):
                nc.scalar.activation(scaled[m // 4][:, blocks[m % 4]], src[:, blocks[n]], COPY, scale=factors[:, n : n + 1])

        turned = [bank("turned0", 4), bank("turned1", 5)]
        turn(turned[0], (0, 1, 2, 3))
        turn(turned[1], (4, 5, 6, 7))
        scale(turned[0], (0, 1, 2, 3), scale_cols)
        nc.scalar.copy(v3a[:, tail], accs[3][:, tail])
        nc.scalar.copy(v3b[:], accs[3][:, second])
        scale(turned[1], (4, 5), spread_cols[:, 4:6])
        back = [bank("back0", 2), bank("back1", 3)]
        for m in range(4):
            nc.tensor.transpose(back[0][:, blocks[m]], scaled[0][:, blocks[m]], identity[:])
        nc.scalar.activation(places(3, first), v3a[:], COPY)
        scale(turned[1][:, HALF:], (6, 7), spread_cols[:, 6:8])
        for m in range(4):
            nc.tensor.transpose(back[1][:, blocks[m]], scaled[1][:, blocks[m]], identity[:])
        nc.scalar.activation(places(3, second), v3b[:], COPY)

        results = [keep.tile([P, T], F32, name=f"result{j}", align_bytes=ROW) for j in range(E_TILES)]
        kept0 = late.tile([P, T], F32, name="kept0", offset=2048)
        nc.gpsimd.tensor_tensor(kept0[:], olds[0][:], retain_wide[:], MULT)
        nc.gpsimd.tensor_tensor(results[0][:], kept0[:], windows[0][:], ADD)
        nc.sync.dma_start(out=out[0:P, :], in_=results[0][:])
        for cols in (halves[0], slice(4 * P, 6 * P), slice(6 * P, T)):
            nc.gpsimd.tensor_tensor(results[1][:, cols], kept1[:, cols], windows[1][:, cols], ADD)
            nc.sync.dma_start(out=out[P : 2 * P, cols], in_=results[1][:, cols])

        own, shared, last = slice(0, 3 * P), slice(3 * P, 6 * P), slice(6 * P, T)
        kept3a = keep.tile([P, 3 * P], F32, name="kept3a", tag="after_turn_back0")
        kept3b = late.tile([P, 3 * P], F32, name="kept3b", offset=6144)
        kept3c = keep.tile([P, HALF], F32, name="kept3c", tag="after_turn_back1")

        def add_back(h):
            nc.vector.tensor_tensor(results[2][:, halves[h]], windows[2][:, halves[h]], back[h][:], ADD)
            nc.sync.dma_start(out=out[2 * P : 3 * P, halves[h]], in_=results[2][:, halves[h]])

        add_back(0)
        nc.vector.tensor_tensor(kept3a[:], olds[3][:, own], spread[0][:, own], MULT)
        add_back(1)
        nc.vector.tensor_tensor(kept3c[:], olds[3][:, last], spread[1][:, HALF:], MULT)
        nc.gpsimd.tensor_tensor(kept3b[:], olds[3][:, shared], retain_wide[:, shared], MULT)
        for kept, cols in ((kept3a[:], own), (kept3b[:], shared), (kept3c[:], last)):
            nc.vector.tensor_tensor(results[3][:, cols], windows[3][:, cols], kept, ADD)
            nc.sync.dma_start(out=out[3 * P : 4 * P, cols], in_=results[3][:, cols])
